import numpy as np
import ml_dtypes


def mxq(x, axis, fmt="e4m3"):
    dtype, down = {"e4m3": (ml_dtypes.float8_e4m3fn, 7), "e5m2": (ml_dtypes.float8_e5m2, 14)}[fmt]
    v = np.moveaxis(np.asarray(x, np.float32).astype(ml_dtypes.bfloat16).astype(np.float64), axis, -1)
    blocks = v.reshape(v.shape[:-1] + (-1, 32))
    amax = np.abs(blocks).max(-1, keepdims=True)
    byte = np.maximum(np.where(amax > 0, np.frexp(amax)[1] - 1 + 127, 0) - down, 1)
    scale = np.exp2(byte - 127.0)
    codes = (blocks / scale).astype(np.float32).astype(dtype).astype(np.float64)
    return np.moveaxis((codes * scale).reshape(v.shape), -1, axis)


WIDE = False


def mx_kscale(k):
    if not WIDE:
        return np.ones(k)
    levels = np.array([10, -10, 5, -5, 0])
    if k % 512:
        return np.exp2(np.random.permutation(np.resize(levels, k // 32))).repeat(32)
    a = np.empty((k // 512, 16))
    for p in range(k // 512):
        a[p, :8] = np.random.permutation(np.resize(levels, 8))
        for g in range(8):
            far = levels[np.abs(levels - a[p, g]) >= 10]
            a[p, g + 8] = far[np.random.randint(len(far))]
    return np.exp2(a.ravel()).repeat(32)


def f64(x):
    return np.asarray(x).astype(np.float64)


def striped(idx):
    return np.tile(idx.reshape(-1, 16).T, (8, 1)).astype(np.uint16)


def unstriped(offs):
    return offs[:16].T.reshape(-1).astype(np.int64)


def pack_weight(w):
    k, n = w.shape
    w = f64(np.asarray(w, np.float32).astype(ml_dtypes.bfloat16)).reshape(k // 32, 32, n)
    amax = np.abs(w).max(1)
    byte = np.clip(np.where(amax > 0, np.frexp(amax)[1] - 1 + 127 - 7, 1), 1, 254)
    scaled = (w * np.exp2(127.0 - byte)[:, None, :]).reshape(k, n).astype(np.float32)
    words = np.ascontiguousarray(scaled.reshape(k // 512, 128, 4, n).transpose(0, 1, 3, 2)).astype(ml_dtypes.float8_e4m3fn).view(np.uint8)
    return words, np.ascontiguousarray(byte.astype(np.uint8).reshape(k // 512, 16, n))


def unpack_weight(words, scales):
    g, p, n, _ = words.shape
    vals = np.ascontiguousarray(words).view(ml_dtypes.float8_e4m3fn).astype(np.float64) * np.repeat(np.exp2(scales.astype(np.float64) - 127.0), 8, axis=1)[..., None]
    return vals.transpose(0, 1, 3, 2).reshape(g * 512, n)


E2M1 = np.array([0.0, 0.5, 1.0, 1.5, 2.0, 3.0, 4.0, 6.0, -0.0, -0.5, -1.0, -1.5, -2.0, -3.0, -4.0, -6.0])


def pack_fp4(w):
    k, n = w.shape
    w = f64(np.asarray(w, np.float32).astype(ml_dtypes.bfloat16)).reshape(k // 32, 32, n)
    amax = np.abs(w).max(1)
    mant, ex = np.frexp(amax / 6.0)
    byte = np.clip(np.where(amax > 0, np.where(mant > 0.5, ex, ex - 1) + 127, 1), 1, 254)
    scaled = (w * np.exp2(127.0 - byte)[:, None, :]).reshape(k, n).astype(np.float32)
    c = np.ascontiguousarray(scaled.reshape(k // 512, 128, 4, n).transpose(0, 1, 3, 2)).astype(ml_dtypes.float4_e2m1fn).view(np.uint8) & 0xF
    words = (c[..., 0::2] | (c[..., 1::2] << 4)).reshape(k // 512, 128, 2 * n)
    return np.ascontiguousarray(words), np.ascontiguousarray(byte.astype(np.uint8).reshape(k // 512, 16, n))


def unpack_fp4(words, scales):
    g, _, n = scales.shape
    words = np.ascontiguousarray(words).reshape(g, 128, n, 2)
    nib = np.empty((g, 128, n, 4), np.uint8)
    nib[..., 0::2] = words & 0xF
    nib[..., 1::2] = words >> 4
    vals = E2M1[nib] * np.repeat(np.exp2(scales.astype(np.float64) - 127.0), 8, axis=1)[..., None]
    return vals.transpose(0, 1, 3, 2).reshape(g * 512, n)


K, T, S, H, N = 512, 2048, 1024, 512, 256


def setup_inputs():
    n = np.random.standard_normal
    s = mx_kscale(K)[:, None]
    u = mx_kscale(H)
    packed_xT = pack_weight(n((K, T)) * s)
    packed_w2 = pack_fp4(n((H, N)) / np.sqrt(H) / u[:, None])
    return {
        "x_words": packed_xT[0],
        "x_scales": packed_xT[1],
        "w1": (n((K, H)) / np.sqrt(K) / s * u).astype(np.float32),
        "w2_words": packed_w2[0],
        "w2_scales": packed_w2[1],
        "pos": (0.5 * n((H, S)) * u[:, None]).astype(np.float32),
        "offs": striped(np.random.permutation(T)[(T * np.random.uniform(0, 1, S) ** 4).astype(np.int64)]),
    }


def reference(x_words, x_scales, w1, w2_words, w2_scales, pos, offs):
    xq = unpack_weight(x_words, x_scales)[:, unstriped(offs)]
    h = (mxq(f64(w1), 0, "e4m3").T @ xq) + f64(pos)
    return unpack_fp4(w2_words, w2_scales).T @ mxq(h, 0, "e4m3")

@@ -1,0 +1,147 @@
+from contextlib import ExitStack
+
+import concourse.mybir as mybir
+
+K, T, S, H, N = 512, 2048, 1024, 512, 256
+FLOPS = 2 * K * H * S + 2 * H * N * S
+
+F32 = mybir.dt.float32
+BF16 = mybir.dt.bfloat16
+I32 = mybir.dt.int32
+U32 = mybir.dt.uint32
+U16 = mybir.dt.uint16
+U8 = mybir.dt.uint8
+FP8X4 = mybir.dt.float8_e4m3fn_x4
+FP4X4 = mybir.dt.float4_e2m1fn_x4
+ADD = mybir.AluOpType.add
+
+P = 128
+PACK = 4
+GROUP = 256
+CHUNK = 128
+W_HALF = H // 2
+
+
+def tile_picked_embpos_none_p_kernel(tc, x_words, x_scales, w1, w2_words, w2_scales, pos, offs, out):
+    nc = tc.nc
+    groups = S // GROUP
+    with ExitStack() as ctx:
+        keep = ctx.enter_context(tc.tile_pool(name="keep", bufs=1))
+        ring = ctx.enter_context(tc.tile_pool(name="ring", bufs=3))
+        psum1 = ctx.enter_context(tc.psum_pool(name="psum1", bufs=5))
+        psum2 = ctx.enter_context(tc.psum_pool(name="psum2", bufs=3))
+
+        offsets = keep.tile([P, S // 16], U16, name="offsets")
+        nc.sync.dma_start(offsets[:], offs)
+
+        xs_table = keep.tile([P, T], U8, name="xs_table", align_bytes=64)
+        nc.vector.memset(xs_table[:].bitcast(I32), 0)
+        for q in range(4):
+            nc.scalar.dma_start(out=xs_table[32 * q : 32 * q + 4, :].bitcast(I32), in_=x_scales[0, 4 * q : 4 * q + 4, :].bitcast(I32))
+
+        w1_rows = w1.rearrange("(p j) c -> p j c", j=PACK)
+        w1_raw = [ring.tile([P, PACK, W_HALF], F32, name="stage", align_bytes=64) for u in range(2)]
+        for u in range(2):
+            nc.sync.dma_start(out=w1_raw[u][:], in_=w1_rows[:, :, u * W_HALF : (u + 1) * W_HALF])
+
+        xw_table = keep.tile([P, T], U32, name="xw_table", align_bytes=64)
+        nc.sync.dma_start(out=xw_table[:].bitcast(I32), in_=x_words[0].rearrange("p n t -> p (n t)").bitcast(I32))
+
+        pos_rows = pos.rearrange("(p t) s -> p t s", t=PACK)
+        pos_sb = []
+
+        def load_pos(g):
+            staged = ring.tile([P, PACK, GROUP], F32, name="stage", align_bytes=64)
+            nc.sync.dma_start(out=staged[:], in_=pos_rows[:, :, g * GROUP : (g + 1) * GROUP])
+            pos_sb.append(staged)
+
+        load_pos(0)
+
+        w2_codes = keep.tile([P, 2 * N], U8, name="w2_codes", align_bytes=64)
+        w2_plane = keep.tile([P, N], U8, name="w2_plane", align_bytes=64)
+        nc.gpsimd.memset(w2_plane[:].bitcast(I32), 0)
+        nc.gpsimd.dma_start(out=w2_codes[:].bitcast(I32), in_=w2_words[0].bitcast(I32))
+        for q in range(4):
+            nc.gpsimd.dma_start(out=w2_plane[32 * q : 32 * q + 4, :].bitcast(I32), in_=w2_scales[0, 4 * q : 4 * q + 4, :].bitcast(I32))
+
+        xs_picked = keep.tile([P, S], U8, name="xs_picked", align_bytes=64)
+        nc.vector.tensor_copy(xs_picked[:], xs_table[:].indirect(offsets[:]))
+
+        w1_bf = keep.tile([P, PACK, P, PACK], BF16, name="w1_bf", align_bytes=64)
+        for u in range(2):
+            nc.scalar.copy(
+                out=w1_bf[:, :, u * 64 : (u + 1) * 64, :].rearrange("p (a e) m j -> p a m j e", e=2),
+                in_=w1_raw[u][:].rearrange("p j (m a e) -> p a m j e", a=2, e=2),
+            )
+        load_pos(1)
+        load_pos(2)
+        w1_codes = keep.tile([P, H], U32, name="w1_codes", align_bytes=64)
+        w1_plane = keep.tile([P, H], U8, name="w1_plane", align_bytes=64)
+        nc.vector.quantize_mx(out=w1_codes[:].bitcast(FP8X4), scales=w1_plane[:], in_=w1_bf[:].rearrange("p t m j -> p (t m j)"))
+
+        xw_picked = [keep.tile([P, GROUP], U32, name=f"xw_picked{g}", align_bytes=64) for g in range(groups)]
+        h_bf = [keep.tile([P, GROUP * PACK], BF16, name=f"h_grp{g}", align_bytes=64) for g in range(groups)]
+        out_rows = out.rearrange("(u p) s -> p u s", p=P)
+
+        def gather(g):
+            cols = GROUP // 16
+            nc.vector.tensor_copy(xw_picked[g][:], xw_table[:].indirect(offsets[:, g * cols : (g + 1) * cols]))
+
+        def layer1(c):
+            g, lo = divmod(c * CHUNK, GROUP)
+            acc = psum1.tile([P, PACK, CHUNK], F32, name="acc1")
+            for t in range(PACK):
+                nc.tensor.matmul_mx(
+                    out=acc[:, t, :],
+                    lhsT=w1_codes[:, t * P : (t + 1) * P].bitcast(FP8X4),
+                    lhsT_scale=w1_plane[:, t * P : (t + 1) * P],
+                    rhs=xw_picked[g][:, lo : lo + CHUNK].bitcast(FP8X4),
+                    rhs_scale=xs_picked[:, c * CHUNK : (c + 1) * CHUNK],
+                    start=True,
+                    stop=True,
+                )
+            nc.vector.tensor_tensor(
+                h_bf[g][:, lo * PACK : (lo + CHUNK) * PACK].rearrange("p (s i t) -> p s t i", i=2, t=PACK),
+                acc[:].rearrange("p t (s i) -> p s t i", i=2),
+                pos_sb[g][:, :, lo : lo + CHUNK].rearrange("p t (s i) -> p s t i", i=2),
+                ADD,
+            )
+
+        def layer2(start, width):
+            g, lo = divmod(start, GROUP)
+            h_codes = keep.tile([P, width], U32, name=f"h_codes{start}", align_bytes=64)
+            h_plane = keep.tile([P, width], U8, name=f"h_plane{start}", align_bytes=64)
+            nc.vector.quantize_mx(out=h_codes[:].bitcast(FP8X4), scales=h_plane[:], in_=h_bf[g][:, lo * PACK : (lo + width) * PACK])
+            acc = psum2.tile([P, 2, width], F32, name="acc2")
+            for u in range(2):
+                nc.tensor.matmul_mx(
+                    out=acc[:, u, :],
+                    lhsT=w2_codes[:, 2 * u * P : 2 * (u + 1) * P].bitcast(FP4X4),
+                    lhsT_scale=w2_plane[:, u * P : (u + 1) * P],
+                    rhs=h_codes[:].bitcast(FP8X4),
+                    rhs_scale=h_plane[:],
+                    start=True,
+                    stop=True,
+                )
+            res = keep.tile([P, 2, width], F32, name=f"res{start}", align_bytes=64)
+            nc.scalar.copy(out=res[:], in_=acc[:])
+            nc.sync.dma_start(out=out_rows[:, :, start : start + width], in_=res[:])
+
+        gather(0)
+        gather(1)
+        layer1(0)
+        layer1(1)
+        load_pos(3)
+        gather(2)
+        layer2(0, GROUP)
+        layer1(2)
+        layer1(3)
+        gather(3)
+        layer2(GROUP, GROUP)
+        layer1(4)
+        layer1(5)
+        layer1(6)
+        layer2(2 * GROUP, GROUP)
+        layer1(7)
+        layer2(3 * GROUP, CHUNK)
+        layer2(3 * GROUP + CHUNK, CHUNK)

@@ -19,7 +19,7 @@ P = 128
 PACK = 4
 GROUP = 256
 CHUNK = 128
-W_HALF = H // 2
+W_CUTS = ((0, 128), (128, 384), (384, 512))
 
 
 def tile_picked_embpos_none_p_kernel(tc, x_words, x_scales, w1, w2_words, w2_scales, pos, offs, out):
@@ -27,7 +27,6 @@ def tile_picked_embpos_none_p_kernel(tc, x_words, x_scales, w1, w2_words, w2_sca
     groups = S // GROUP
     with ExitStack() as ctx:
         keep = ctx.enter_context(tc.tile_pool(name="keep", bufs=1))
-        ring = ctx.enter_context(tc.tile_pool(name="ring", bufs=3))
         psum1 = ctx.enter_context(tc.psum_pool(name="psum1", bufs=5))
         psum2 = ctx.enter_context(tc.psum_pool(name="psum2", bufs=3))
 
@@ -36,55 +35,54 @@ def tile_picked_embpos_none_p_kernel(tc, x_words, x_scales, w1, w2_words, w2_sca
 
         xs_table = keep.tile([P, T], U8, name="xs_table", align_bytes=64)
         nc.vector.memset(xs_table[:].bitcast(I32), 0)
-        for q in range(4):
-            nc.scalar.dma_start(out=xs_table[32 * q : 32 * q + 4, :].bitcast(I32), in_=x_scales[0, 4 * q : 4 * q + 4, :].bitcast(I32))
+        w2_plane = keep.tile([P, N], U8, name="w2_plane", align_bytes=64)
+        nc.vector.memset(w2_plane[:].bitcast(I32), 0)
 
         w1_rows = w1.rearrange("(p j) c -> p j c", j=PACK)
-        w1_raw = [ring.tile([P, PACK, W_HALF], F32, name="stage", align_bytes=64) for u in range(2)]
-        for u in range(2):
-            nc.sync.dma_start(out=w1_raw[u][:], in_=w1_rows[:, :, u * W_HALF : (u + 1) * W_HALF])
+        w1_raw = [keep.tile([P, PACK, hi - lo], F32, name=f"w1_raw{lo}", align_bytes=64) for lo, hi in W_CUTS]
 
+        def load_w1(u):
+            lo, hi = W_CUTS[u]
+            nc.sync.dma_start(out=w1_raw[u][:], in_=w1_rows[:, :, lo:hi])
+
+        load_w1(0)
+        for q in range(4):
+            nc.sync.dma_start(out=xs_table[32 * q : 32 * q + 4, :].bitcast(I32), in_=x_scales[0, 4 * q : 4 * q + 4, :].bitcast(I32))
         xw_table = keep.tile([P, T], U32, name="xw_table", align_bytes=64)
         nc.sync.dma_start(out=xw_table[:].bitcast(I32), in_=x_words[0].rearrange("p n t -> p (n t)").bitcast(I32))
+        load_w1(1)
+        load_w1(2)
 
         pos_rows = pos.rearrange("(p t) s -> p t s", t=PACK)
-        pos_sb = []
-
-        def load_pos(g):
-            staged = ring.tile([P, PACK, GROUP], F32, name="stage", align_bytes=64)
-            nc.sync.dma_start(out=staged[:], in_=pos_rows[:, :, g * GROUP : (g + 1) * GROUP])
-            pos_sb.append(staged)
-
-        load_pos(0)
+        pos_sb = [keep.tile([P, PACK, GROUP], F32, name=f"pos{g}", align_bytes=64) for g in range(groups)]
+        nc.sync.dma_start(out=pos_sb[0][:], in_=pos_rows[:, :, 0:GROUP])
 
         w2_codes = keep.tile([P, 2 * N], U8, name="w2_codes", align_bytes=64)
-        w2_plane = keep.tile([P, N], U8, name="w2_plane", align_bytes=64)
-        nc.gpsimd.memset(w2_plane[:].bitcast(I32), 0)
-        nc.gpsimd.dma_start(out=w2_codes[:].bitcast(I32), in_=w2_words[0].bitcast(I32))
+        nc.sync.dma_start(out=w2_codes[:].bitcast(I32), in_=w2_words[0].bitcast(I32))
         for q in range(4):
-            nc.gpsimd.dma_start(out=w2_plane[32 * q : 32 * q + 4, :].bitcast(I32), in_=w2_scales[0, 4 * q : 4 * q + 4, :].bitcast(I32))
+            nc.sync.dma_start(out=w2_plane[32 * q : 32 * q + 4, :].bitcast(I32), in_=w2_scales[0, 4 * q : 4 * q + 4, :].bitcast(I32))
+        for g in range(1, groups):
+            nc.sync.dma_start(out=pos_sb[g][:], in_=pos_rows[:, :, g * GROUP : (g + 1) * GROUP])
 
         xs_picked = keep.tile([P, S], U8, name="xs_picked", align_bytes=64)
         nc.vector.tensor_copy(xs_picked[:], xs_table[:].indirect(offsets[:]))
 
-        w1_bf = keep.tile([P, PACK, P, PACK], BF16, name="w1_bf", align_bytes=64)
-        for u in range(2):
+        w1_bf = keep.tile([P, PACK, P, PACK], BF16, name="shared", align_bytes=64)
+        for u, (lo, hi) in enumerate(W_CUTS):
             nc.scalar.copy(
-                out=w1_bf[:, :, u * 64 : (u + 1) * 64, :].rearrange("p (a e) m j -> p a m j e", e=2),
+                out=w1_bf[:, :, lo // PACK : hi // PACK, :].rearrange("p (a e) m j -> p a m j e", e=2),
                 in_=w1_raw[u][:].rearrange("p j (m a e) -> p a m j e", a=2, e=2),
             )
-        load_pos(1)
-        load_pos(2)
-        w1_codes = keep.tile([P, H], U32, name="w1_codes", align_bytes=64)
-        w1_plane = keep.tile([P, H], U8, name="w1_plane", align_bytes=64)
-        nc.vector.quantize_mx(out=w1_codes[:].bitcast(FP8X4), scales=w1_plane[:], in_=w1_bf[:].rearrange("p t m j -> p (t m j)"))
+        w1_codes = [keep.tile([P, P], U32, name=f"w1_codes{t}", align_bytes=64) for t in range(PACK)]
+        w1_plane = [keep.tile([P, P], U8, name=f"w1_plane{t}", align_bytes=64) for t in range(PACK)]
 
-        xw_picked = [keep.tile([P, GROUP], U32, name=f"xw_picked{g}", align_bytes=64) for g in range(groups)]
+        xw_picked = []
         h_bf = [keep.tile([P, GROUP * PACK], BF16, name=f"h_grp{g}", align_bytes=64) for g in range(groups)]
         out_rows = out.rearrange("(u p) s -> p u s", p=P)
 
         def gather(g):
             cols = GROUP // 16
+            xw_picked.append(keep.tile([P, GROUP], U32, name="shared" if g == groups - 1 else f"xw_picked{g}", align_bytes=64))
             nc.vector.tensor_copy(xw_picked[g][:], xw_table[:].indirect(offsets[:, g * cols : (g + 1) * cols]))
 
         def layer1(c):
@@ -93,8 +91,8 @@ def tile_picked_embpos_none_p_kernel(tc, x_words, x_scales, w1, w2_words, w2_sca
             for t in range(PACK):
                 nc.tensor.matmul_mx(
                     out=acc[:, t, :],
-                    lhsT=w1_codes[:, t * P : (t + 1) * P].bitcast(FP8X4),
-                    lhsT_scale=w1_plane[:, t * P : (t + 1) * P],
+                    lhsT=w1_codes[t][:].bitcast(FP8X4),
+                    lhsT_scale=w1_plane[t][:],
                     rhs=xw_picked[g][:, lo : lo + CHUNK].bitcast(FP8X4),
                     rhs_scale=xs_picked[:, c * CHUNK : (c + 1) * CHUNK],
                     start=True,
@@ -112,10 +110,15 @@ def tile_picked_embpos_none_p_kernel(tc, x_words, x_scales, w1, w2_words, w2_sca
             h_codes = keep.tile([P, width], U32, name=f"h_codes{start}", align_bytes=64)
             h_plane = keep.tile([P, width], U8, name=f"h_plane{start}", align_bytes=64)
             nc.vector.quantize_mx(out=h_codes[:].bitcast(FP8X4), scales=h_plane[:], in_=h_bf[g][:, lo * PACK : (lo + width) * PACK])
-            acc = psum2.tile([P, 2, width], F32, name="acc2")
+            last = start + width == S
+            if last:
+                accs = [psum2.tile([P, width], F32, name="acc2")[:] for u in range(2)]
+            else:
+                both = psum2.tile([P, 2, width], F32, name="acc2")
+                accs = [both[:, u, :] for u in range(2)]
             for u in range(2):
                 nc.tensor.matmul_mx(
-                    out=acc[:, u, :],
+                    out=accs[u],
                     lhsT=w2_codes[:, 2 * u * P : 2 * (u + 1) * P].bitcast(FP4X4),
                     lhsT_scale=w2_plane[:, u * P : (u + 1) * P],
                     rhs=h_codes[:].bitcast(FP8X4),
@@ -123,22 +126,29 @@ def tile_picked_embpos_none_p_kernel(tc, x_words, x_scales, w1, w2_words, w2_sca
                     start=True,
                     stop=True,
                 )
-            res = keep.tile([P, 2, width], F32, name=f"res{start}", align_bytes=64)
-            nc.scalar.copy(out=res[:], in_=acc[:])
-            nc.sync.dma_start(out=out_rows[:, :, start : start + width], in_=res[:])
+            if last:
+                res = [keep.tile([P, width], F32, name=f"res_last{u}", align_bytes=64) for u in range(2)]
+                nc.scalar.copy(out=res[0][:], in_=accs[0])
+                nc.scalar.dma_start(out=out_rows[:, 0, start : start + width], in_=res[0][:])
+                nc.vector.tensor_copy(out=res[1][:], in_=accs[1])
+                nc.sync.dma_start(out=out_rows[:, 1, start : start + width], in_=res[1][:])
+            else:
+                res = keep.tile([P, 2, width], F32, name=f"res{start}", align_bytes=64)
+                nc.scalar.copy(out=res[:], in_=both[:])
+                nc.sync.dma_start(out=out_rows[:, :, start : start + width], in_=res[:])
 
-        gather(0)
-        gather(1)
+        for g in range(groups - 1):
+            gather(g)
+        for t in range(PACK):
+            nc.vector.quantize_mx(out=w1_codes[t][:].bitcast(FP8X4), scales=w1_plane[t][:], in_=w1_bf[:, t, :, :].rearrange("p m j -> p (m j)"))
+        gather(groups - 1)
         layer1(0)
         layer1(1)
-        load_pos(3)
-        gather(2)
-        layer2(0, GROUP)
         layer1(2)
+        layer2(0, GROUP)
         layer1(3)
-        gather(3)
-        layer2(GROUP, GROUP)
         layer1(4)
+        layer2(GROUP, GROUP)
         layer1(5)
         layer1(6)
         layer2(2 * GROUP, GROUP)

@@ -19,7 +19,9 @@ P = 128
 PACK = 4
 GROUP = 256
 CHUNK = 128
-W_CUTS = ((0, 128), (128, 384), (384, 512))
+W_CUTS = ((0, 256), (256, 384), (384, 512))
+SIDE_CHUNKS = ()
+BANKS = 4
 
 
 def tile_picked_embpos_none_p_kernel(tc, x_words, x_scales, w1, w2_words, w2_scales, pos, offs, out):
@@ -27,8 +29,8 @@ def tile_picked_embpos_none_p_kernel(tc, x_words, x_scales, w1, w2_words, w2_sca
     groups = S // GROUP
     with ExitStack() as ctx:
         keep = ctx.enter_context(tc.tile_pool(name="keep", bufs=1))
-        psum1 = ctx.enter_context(tc.psum_pool(name="psum1", bufs=5))
-        psum2 = ctx.enter_context(tc.psum_pool(name="psum2", bufs=3))
+        psum1 = ctx.enter_context(tc.psum_pool(name="psum1", bufs=BANKS))
+        psum2 = ctx.enter_context(tc.psum_pool(name="psum2", bufs=BANKS))
 
         offsets = keep.tile([P, S // 16], U16, name="offsets")
         nc.sync.dma_start(offsets[:], offs)
@@ -47,7 +49,7 @@ def tile_picked_embpos_none_p_kernel(tc, x_words, x_scales, w1, w2_words, w2_sca
 
         load_w1(0)
         for q in range(4):
-            nc.sync.dma_start(out=xs_table[32 * q : 32 * q + 4, :].bitcast(I32), in_=x_scales[0, 4 * q : 4 * q + 4, :].bitcast(I32))
+            nc.sync.dma_start(out=xs_table[q:P:32, :].bitcast(I32), in_=x_scales[0, q:16:4, :].bitcast(I32))
         xw_table = keep.tile([P, T], U32, name="xw_table", align_bytes=64)
         nc.sync.dma_start(out=xw_table[:].bitcast(I32), in_=x_words[0].rearrange("p n t -> p (n t)").bitcast(I32))
         load_w1(1)
@@ -60,7 +62,7 @@ def tile_picked_embpos_none_p_kernel(tc, x_words, x_scales, w1, w2_words, w2_sca
         w2_codes = keep.tile([P, 2 * N], U8, name="w2_codes", align_bytes=64)
         nc.sync.dma_start(out=w2_codes[:].bitcast(I32), in_=w2_words[0].bitcast(I32))
         for q in range(4):
-            nc.sync.dma_start(out=w2_plane[32 * q : 32 * q + 4, :].bitcast(I32), in_=w2_scales[0, 4 * q : 4 * q + 4, :].bitcast(I32))
+            nc.sync.dma_start(out=w2_plane[q:P:32, :].bitcast(I32), in_=w2_scales[0, q:16:4, :].bitcast(I32))
         for g in range(1, groups):
             nc.sync.dma_start(out=pos_sb[g][:], in_=pos_rows[:, :, g * GROUP : (g + 1) * GROUP])
 
@@ -73,8 +75,8 @@ def tile_picked_embpos_none_p_kernel(tc, x_words, x_scales, w1, w2_words, w2_sca
                 out=w1_bf[:, :, lo // PACK : hi // PACK, :].rearrange("p (a e) m j -> p a m j e", e=2),
                 in_=w1_raw[u][:].rearrange("p j (m a e) -> p a m j e", a=2, e=2),
             )
-        w1_codes = [keep.tile([P, P], U32, name=f"w1_codes{t}", align_bytes=64) for t in range(PACK)]
-        w1_plane = [keep.tile([P, P], U8, name=f"w1_plane{t}", align_bytes=64) for t in range(PACK)]
+        w1_codes = [keep.tile([P, 2 * P], U32, name=f"w1_codes{a}", align_bytes=64) for a in range(2)]
+        w1_plane = [keep.tile([P, 2 * P], U8, name=f"w1_plane{a}", align_bytes=64) for a in range(2)]
 
         xw_picked = []
         h_bf = [keep.tile([P, GROUP * PACK], BF16, name=f"h_grp{g}", align_bytes=64) for g in range(groups)]
@@ -85,19 +87,41 @@ def tile_picked_embpos_none_p_kernel(tc, x_words, x_scales, w1, w2_words, w2_sca
             xw_picked.append(keep.tile([P, GROUP], U32, name="shared" if g == groups - 1 else f"xw_picked{g}", align_bytes=64))
             nc.vector.tensor_copy(xw_picked[g][:], xw_table[:].indirect(offsets[:, g * cols : (g + 1) * cols]))
 
-        def layer1(c):
+        accs1 = []
+
+        def project(c):
             g, lo = divmod(c * CHUNK, GROUP)
             acc = psum1.tile([P, PACK, CHUNK], F32, name="acc1")
+            accs1.append(acc)
             for t in range(PACK):
                 nc.tensor.matmul_mx(
                     out=acc[:, t, :],
-                    lhsT=w1_codes[t][:].bitcast(FP8X4),
-                    lhsT_scale=w1_plane[t][:],
+                    lhsT=w1_codes[t // 2][:, t % 2 * P : (t % 2 + 1) * P].bitcast(FP8X4),
+                    lhsT_scale=w1_plane[t // 2][:, t % 2 * P : (t % 2 + 1) * P],
                     rhs=xw_picked[g][:, lo : lo + CHUNK].bitcast(FP8X4),
                     rhs_scale=xs_picked[:, c * CHUNK : (c + 1) * CHUNK],
                     start=True,
                     stop=True,
                 )
+
+        def add_pos(c):
+            add_only(c)
+            if c + BANKS < S // CHUNK:
+                project(c + BANKS)
+
+        def add_only(c):
+            g, lo = divmod(c * CHUNK, GROUP)
+            acc = accs1[c]
+            if c in SIDE_CHUNKS:
+                staged = keep.tile([P, CHUNK, PACK], F32, name=f"staged{c}", align_bytes=64)
+                nc.scalar.copy(out=staged[:], in_=acc[:].rearrange("p t s -> p s t"))
+                nc.gpsimd.tensor_tensor(
+                    h_bf[g][:, lo * PACK : (lo + CHUNK) * PACK].rearrange("p (s t) -> p s t", t=PACK),
+                    staged[:],
+                    pos_sb[g][:, :, lo : lo + CHUNK].rearrange("p t s -> p s t"),
+                    ADD,
+                )
+                return
             nc.vector.tensor_tensor(
                 h_bf[g][:, lo * PACK : (lo + CHUNK) * PACK].rearrange("p (s i t) -> p s t i", i=2, t=PACK),
                 acc[:].rearrange("p t (s i) -> p s t i", i=2),
@@ -139,19 +163,21 @@ def tile_picked_embpos_none_p_kernel(tc, x_words, x_scales, w1, w2_words, w2_sca
 
         for g in range(groups - 1):
             gather(g)
-        for t in range(PACK):
-            nc.vector.quantize_mx(out=w1_codes[t][:].bitcast(FP8X4), scales=w1_plane[t][:], in_=w1_bf[:, t, :, :].rearrange("p m j -> p (m j)"))
+        for a in range(2):
+            nc.vector.quantize_mx(out=w1_codes[a][:].bitcast(FP8X4), scales=w1_plane[a][:], in_=w1_bf[:, 2 * a : 2 * a + 2, :, :].rearrange("p t m j -> p (t m j)"))
         gather(groups - 1)
-        layer1(0)
-        layer1(1)
-        layer1(2)
-        layer2(0, GROUP)
-        layer1(3)
-        layer1(4)
-        layer2(GROUP, GROUP)
-        layer1(5)
-        layer1(6)
-        layer2(2 * GROUP, GROUP)
-        layer1(7)
-        layer2(3 * GROUP, CHUNK)
-        layer2(3 * GROUP + CHUNK, CHUNK)
+        for c in range(BANKS):
+            project(c)
+        add_pos(0)
+        add_pos(1)
+        add_pos(2)
+        layer2(0 * CHUNK, GROUP)
+        add_pos(3)
+        add_pos(4)
+        layer2(2 * CHUNK, GROUP)
+        add_pos(5)
+        add_pos(6)
+        layer2(4 * CHUNK, GROUP)
+        add_pos(7)
+        layer2(6 * CHUNK, CHUNK)
+        layer2(7 * CHUNK, CHUNK)

@@ -22,6 +22,7 @@ CHUNK = 128
 W_CUTS = ((0, 256), (256, 384), (384, 512))
 SIDE_CHUNKS = ()
 BANKS = 4
+PIECES = ((0, 256), (256, 256), (512, 256), (768, 128), (896, 128))
 
 
 def tile_picked_embpos_none_p_kernel(tc, x_words, x_scales, w1, w2_words, w2_scales, pos, offs, out):
@@ -57,13 +58,14 @@ def tile_picked_embpos_none_p_kernel(tc, x_words, x_scales, w1, w2_words, w2_sca
 
         pos_rows = pos.rearrange("(p t) s -> p t s", t=PACK)
         pos_sb = [keep.tile([P, PACK, GROUP], F32, name=f"pos{g}", align_bytes=64) for g in range(groups)]
-        nc.sync.dma_start(out=pos_sb[0][:], in_=pos_rows[:, :, 0:GROUP])
+        for g in range(2):
+            nc.sync.dma_start(out=pos_sb[g][:], in_=pos_rows[:, :, g * GROUP : (g + 1) * GROUP])
 
         w2_codes = keep.tile([P, 2 * N], U8, name="w2_codes", align_bytes=64)
         nc.sync.dma_start(out=w2_codes[:].bitcast(I32), in_=w2_words[0].bitcast(I32))
         for q in range(4):
-            nc.sync.dma_start(out=w2_plane[q:P:32, :].bitcast(I32), in_=w2_scales[0, q:16:4, :].bitcast(I32))
-        for g in range(1, groups):
+            nc.gpsimd.dma_start(out=w2_plane[q:P:32, :].bitcast(I32), in_=w2_scales[0, q:16:4, :].bitcast(I32))
+        for g in range(2, groups):
             nc.sync.dma_start(out=pos_sb[g][:], in_=pos_rows[:, :, g * GROUP : (g + 1) * GROUP])
 
         xs_picked = keep.tile([P, S], U8, name="xs_picked", align_bytes=64)
@@ -79,7 +81,13 @@ def tile_picked_embpos_none_p_kernel(tc, x_words, x_scales, w1, w2_words, w2_sca
         w1_plane = [keep.tile([P, 2 * P], U8, name=f"w1_plane{a}", align_bytes=64) for a in range(2)]
 
         xw_picked = []
-        h_bf = [keep.tile([P, GROUP * PACK], BF16, name=f"h_grp{g}", align_bytes=64) for g in range(groups)]
+        h_bf = {start: keep.tile([P, width * PACK], BF16, name=f"h_bf{start}", align_bytes=64) for start, width in PIECES}
+
+        def h_slot(c):
+            start = max(s for s, w in PIECES if s <= c * CHUNK)
+            lo = c * CHUNK - start
+            return h_bf[start][:, lo * PACK : (lo + CHUNK) * PACK]
+
         out_rows = out.rearrange("(u p) s -> p u s", p=P)
 
         def gather(g):
@@ -116,26 +124,25 @@ def tile_picked_embpos_none_p_kernel(tc, x_words, x_scales, w1, w2_words, w2_sca
                 staged = keep.tile([P, CHUNK, PACK], F32, name=f"staged{c}", align_bytes=64)
                 nc.scalar.copy(out=staged[:], in_=acc[:].rearrange("p t s -> p s t"))
                 nc.gpsimd.tensor_tensor(
-                    h_bf[g][:, lo * PACK : (lo + CHUNK) * PACK].rearrange("p (s t) -> p s t", t=PACK),
+                    h_slot(c).rearrange("p (s t) -> p s t", t=PACK),
                     staged[:],
                     pos_sb[g][:, :, lo : lo + CHUNK].rearrange("p t s -> p s t"),
                     ADD,
                 )
                 return
             nc.vector.tensor_tensor(
-                h_bf[g][:, lo * PACK : (lo + CHUNK) * PACK].rearrange("p (s i t) -> p s t i", i=2, t=PACK),
+                h_slot(c).rearrange("p (s i t) -> p s t i", i=2, t=PACK),
                 acc[:].rearrange("p t (s i) -> p s t i", i=2),
                 pos_sb[g][:, :, lo : lo + CHUNK].rearrange("p t (s i) -> p s t i", i=2),
                 ADD,
             )
 
         def layer2(start, width):
-            g, lo = divmod(start, GROUP)
             h_codes = keep.tile([P, width], U32, name=f"h_codes{start}", align_bytes=64)
             h_plane = keep.tile([P, width], U8, name=f"h_plane{start}", align_bytes=64)
-            nc.vector.quantize_mx(out=h_codes[:].bitcast(FP8X4), scales=h_plane[:], in_=h_bf[g][:, lo * PACK : (lo + width) * PACK])
+            nc.vector.quantize_mx(out=h_codes[:].bitcast(FP8X4), scales=h_plane[:], in_=h_bf[start][:])
             last = start + width == S
-            if last:
+            if last or width > GROUP:
                 accs = [psum2.tile([P, width], F32, name="acc2")[:] for u in range(2)]
             else:
                 both = psum2.tile([P, 2, width], F32, name="acc2")
@@ -156,6 +163,11 @@ def tile_picked_embpos_none_p_kernel(tc, x_words, x_scales, w1, w2_words, w2_sca
                 nc.scalar.dma_start(out=out_rows[:, 0, start : start + width], in_=res[0][:])
                 nc.vector.tensor_copy(out=res[1][:], in_=accs[1])
                 nc.sync.dma_start(out=out_rows[:, 1, start : start + width], in_=res[1][:])
+            elif width > GROUP:
+                for u in range(2):
+                    res = keep.tile([P, width], F32, name=f"res_wide{u}", align_bytes=64)
+                    nc.scalar.copy(out=res[:], in_=accs[u])
+                    nc.sync.dma_start(out=out_rows[:, u, start : start + width], in_=res[:])
             else:
                 res = keep.tile([P, 2, width], F32, name=f"res{start}", align_bytes=64)
                 nc.scalar.copy(out=res[:], in_=both[:])
@@ -171,13 +183,13 @@ def tile_picked_embpos_none_p_kernel(tc, x_words, x_scales, w1, w2_words, w2_sca
         add_pos(0)
         add_pos(1)
         add_pos(2)
-        layer2(0 * CHUNK, GROUP)
+        layer2(*PIECES[0])
         add_pos(3)
         add_pos(4)
-        layer2(2 * CHUNK, GROUP)
+        layer2(*PIECES[1])
         add_pos(5)
         add_pos(6)
-        layer2(4 * CHUNK, GROUP)
+        layer2(*PIECES[2])
         add_pos(7)
-        layer2(6 * CHUNK, CHUNK)
-        layer2(7 * CHUNK, CHUNK)
+        layer2(*PIECES[3])
+        layer2(*PIECES[4])

@@ -17,10 +17,12 @@ ADD = mybir.AluOpType.add
 
 P = 128
 PACK = 4
+QUADRANT = 32
+BLOCKS = K // 32
+LIST_ROWS = 16
+W_HALF = H // 2
 GROUP = 256
 CHUNK = 128
-W_CUTS = ((0, 256), (256, 384), (384, 512))
-SIDE_CHUNKS = ()
 BANKS = 4
 PIECES = ((0, 256), (256, 256), (512, 256), (768, 128), (896, 128))
 
@@ -28,12 +30,13 @@ PIECES = ((0, 256), (256, 256), (512, 256), (768, 128), (896, 128))
 def tile_picked_embpos_none_p_kernel(tc, x_words, x_scales, w1, w2_words, w2_scales, pos, offs, out):
     nc = tc.nc
     groups = S // GROUP
+    chunks = S // CHUNK
     with ExitStack() as ctx:
         keep = ctx.enter_context(tc.tile_pool(name="keep", bufs=1))
         psum1 = ctx.enter_context(tc.psum_pool(name="psum1", bufs=BANKS))
         psum2 = ctx.enter_context(tc.psum_pool(name="psum2", bufs=BANKS))
 
-        offsets = keep.tile([P, S // 16], U16, name="offsets")
+        offsets = keep.tile([P, S // LIST_ROWS], U16, name="offsets")
         nc.sync.dma_start(offsets[:], offs)
 
         xs_table = keep.tile([P, T], U8, name="xs_table", align_bytes=64)
@@ -41,71 +44,59 @@ def tile_picked_embpos_none_p_kernel(tc, x_words, x_scales, w1, w2_words, w2_sca
         w2_plane = keep.tile([P, N], U8, name="w2_plane", align_bytes=64)
         nc.vector.memset(w2_plane[:].bitcast(I32), 0)
 
+        def load_plane(plane, scales):
+            for r in range(4):
+                nc.sync.dma_start(out=plane[r:P:QUADRANT, :].bitcast(I32), in_=scales[0, r:BLOCKS:4, :].bitcast(I32))
+
         w1_rows = w1.rearrange("(p j) c -> p j c", j=PACK)
-        w1_raw = [keep.tile([P, PACK, hi - lo], F32, name=f"w1_raw{lo}", align_bytes=64) for lo, hi in W_CUTS]
-
-        def load_w1(u):
-            lo, hi = W_CUTS[u]
-            nc.sync.dma_start(out=w1_raw[u][:], in_=w1_rows[:, :, lo:hi])
-
-        load_w1(0)
-        for q in range(4):
-            nc.sync.dma_start(out=xs_table[q:P:32, :].bitcast(I32), in_=x_scales[0, q:16:4, :].bitcast(I32))
+        w1_raw = [keep.tile([P, PACK, W_HALF], F32, name=f"w1_raw{half}", align_bytes=64) for half in range(2)]
+        nc.sync.dma_start(out=w1_raw[0][:], in_=w1_rows[:, :, :W_HALF])
+        load_plane(xs_table, x_scales)
+        nc.sync.dma_start(out=w1_raw[1][:], in_=w1_rows[:, :, W_HALF:])
         xw_table = keep.tile([P, T], U32, name="xw_table", align_bytes=64)
         nc.sync.dma_start(out=xw_table[:].bitcast(I32), in_=x_words[0].rearrange("p n t -> p (n t)").bitcast(I32))
-        load_w1(1)
-        load_w1(2)
 
         pos_rows = pos.rearrange("(p t) s -> p t s", t=PACK)
         pos_sb = [keep.tile([P, PACK, GROUP], F32, name=f"pos{g}", align_bytes=64) for g in range(groups)]
-        for g in range(2):
-            nc.sync.dma_start(out=pos_sb[g][:], in_=pos_rows[:, :, g * GROUP : (g + 1) * GROUP])
-
         w2_codes = keep.tile([P, 2 * N], U8, name="w2_codes", align_bytes=64)
-        nc.sync.dma_start(out=w2_codes[:].bitcast(I32), in_=w2_words[0].bitcast(I32))
-        for q in range(4):
-            nc.gpsimd.dma_start(out=w2_plane[q:P:32, :].bitcast(I32), in_=w2_scales[0, q:16:4, :].bitcast(I32))
-        for g in range(2, groups):
+        for g in range(groups):
+            if g == groups // 2:
+                nc.sync.dma_start(out=w2_codes[:].bitcast(I32), in_=w2_words[0].bitcast(I32))
+                load_plane(w2_plane, w2_scales)
             nc.sync.dma_start(out=pos_sb[g][:], in_=pos_rows[:, :, g * GROUP : (g + 1) * GROUP])
 
         xs_picked = keep.tile([P, S], U8, name="xs_picked", align_bytes=64)
         nc.vector.tensor_copy(xs_picked[:], xs_table[:].indirect(offsets[:]))
 
-        w1_bf = keep.tile([P, PACK, P, PACK], BF16, name="shared", align_bytes=64)
-        for u, (lo, hi) in enumerate(W_CUTS):
+        w1_bf = keep.tile([P, PACK, P, PACK], BF16, name="w1_bf", align_bytes=64)
+        m_half = W_HALF // PACK
+        for half in range(2):
             nc.scalar.copy(
-                out=w1_bf[:, :, lo // PACK : hi // PACK, :].rearrange("p (a e) m j -> p a m j e", e=2),
-                in_=w1_raw[u][:].rearrange("p j (m a e) -> p a m j e", a=2, e=2),
+                out=w1_bf[:, :, half * m_half : (half + 1) * m_half, :].rearrange("p (a e) m j -> p a m j e", e=2),
+                in_=w1_raw[half][:].rearrange("p j (m a e) -> p a m j e", a=2, e=2),
             )
-        w1_codes = [keep.tile([P, 2 * P], U32, name=f"w1_codes{a}", align_bytes=64) for a in range(2)]
-        w1_plane = [keep.tile([P, 2 * P], U8, name=f"w1_plane{a}", align_bytes=64) for a in range(2)]
+        w1_codes = keep.tile([P, H], U32, name="w1_codes", align_bytes=64)
+        w1_plane = keep.tile([P, H], U8, name="w1_plane", align_bytes=64)
+        nc.vector.quantize_mx(out=w1_codes[:].bitcast(FP8X4), scales=w1_plane[:], in_=w1_bf[:].rearrange("p t m j -> p (t m j)"))
 
-        xw_picked = []
+        xw_picked = [keep.tile([P, GROUP], U32, name=f"xw_picked{g}", align_bytes=64) for g in range(groups)]
+        list_cols = GROUP // LIST_ROWS
+        for g in range(groups):
+            nc.vector.tensor_copy(xw_picked[g][:], xw_table[:].indirect(offsets[:, g * list_cols : (g + 1) * list_cols]))
+
         h_bf = {start: keep.tile([P, width * PACK], BF16, name=f"h_bf{start}", align_bytes=64) for start, width in PIECES}
-
-        def h_slot(c):
-            start = max(s for s, w in PIECES if s <= c * CHUNK)
-            lo = c * CHUNK - start
-            return h_bf[start][:, lo * PACK : (lo + CHUNK) * PACK]
-
         out_rows = out.rearrange("(u p) s -> p u s", p=P)
-
-        def gather(g):
-            cols = GROUP // 16
-            xw_picked.append(keep.tile([P, GROUP], U32, name="shared" if g == groups - 1 else f"xw_picked{g}", align_bytes=64))
-            nc.vector.tensor_copy(xw_picked[g][:], xw_table[:].indirect(offsets[:, g * cols : (g + 1) * cols]))
-
-        accs1 = []
+        projected = []
 
         def project(c):
             g, lo = divmod(c * CHUNK, GROUP)
-            acc = psum1.tile([P, PACK, CHUNK], F32, name="acc1")
-            accs1.append(acc)
+            acc1 = psum1.tile([P, PACK, CHUNK], F32, name="acc1")
+            projected.append(acc1)
             for t in range(PACK):
                 nc.tensor.matmul_mx(
-                    out=acc[:, t, :],
-                    lhsT=w1_codes[t // 2][:, t % 2 * P : (t % 2 + 1) * P].bitcast(FP8X4),
-                    lhsT_scale=w1_plane[t // 2][:, t % 2 * P : (t % 2 + 1) * P],
+                    out=acc1[:, t, :],
+                    lhsT=w1_codes[:, t * P : (t + 1) * P].bitcast(FP8X4),
+                    lhsT_scale=w1_plane[:, t * P : (t + 1) * P],
                     rhs=xw_picked[g][:, lo : lo + CHUNK].bitcast(FP8X4),
                     rhs_scale=xs_picked[:, c * CHUNK : (c + 1) * CHUNK],
                     start=True,
@@ -113,43 +104,29 @@ def tile_picked_embpos_none_p_kernel(tc, x_words, x_scales, w1, w2_words, w2_sca
                 )
 
         def add_pos(c):
-            add_only(c)
-            if c + BANKS < S // CHUNK:
-                project(c + BANKS)
-
-        def add_only(c):
             g, lo = divmod(c * CHUNK, GROUP)
-            acc = accs1[c]
-            if c in SIDE_CHUNKS:
-                staged = keep.tile([P, CHUNK, PACK], F32, name=f"staged{c}", align_bytes=64)
-                nc.scalar.copy(out=staged[:], in_=acc[:].rearrange("p t s -> p s t"))
-                nc.gpsimd.tensor_tensor(
-                    h_slot(c).rearrange("p (s t) -> p s t", t=PACK),
-                    staged[:],
-                    pos_sb[g][:, :, lo : lo + CHUNK].rearrange("p t s -> p s t"),
-                    ADD,
-                )
-                return
+            start = max(first for first, width in PIECES if first <= c * CHUNK)
+            at = (c * CHUNK - start) * PACK
             nc.vector.tensor_tensor(
-                h_slot(c).rearrange("p (s i t) -> p s t i", i=2, t=PACK),
-                acc[:].rearrange("p t (s i) -> p s t i", i=2),
-                pos_sb[g][:, :, lo : lo + CHUNK].rearrange("p t (s i) -> p s t i", i=2),
+                h_bf[start][:, at : at + CHUNK * PACK].rearrange("p (n i t) -> p n t i", i=2, t=PACK),
+                projected[c][:].rearrange("p t (n i) -> p n t i", i=2),
+                pos_sb[g][:, :, lo : lo + CHUNK].rearrange("p t (n i) -> p n t i", i=2),
                 ADD,
             )
 
-        def layer2(start, width):
+        def second_layer(start, width):
             h_codes = keep.tile([P, width], U32, name=f"h_codes{start}", align_bytes=64)
             h_plane = keep.tile([P, width], U8, name=f"h_plane{start}", align_bytes=64)
             nc.vector.quantize_mx(out=h_codes[:].bitcast(FP8X4), scales=h_plane[:], in_=h_bf[start][:])
             last = start + width == S
-            if last or width > GROUP:
-                accs = [psum2.tile([P, width], F32, name="acc2")[:] for u in range(2)]
+            if last:
+                halves = [psum2.tile([P, width], F32, name="acc2")[:] for u in range(2)]
             else:
                 both = psum2.tile([P, 2, width], F32, name="acc2")
-                accs = [both[:, u, :] for u in range(2)]
+                halves = [both[:, u, :] for u in range(2)]
             for u in range(2):
                 nc.tensor.matmul_mx(
-                    out=accs[u],
+                    out=halves[u],
                     lhsT=w2_codes[:, 2 * u * P : 2 * (u + 1) * P].bitcast(FP4X4),
                     lhsT_scale=w2_plane[:, u * P : (u + 1) * P],
                     rhs=h_codes[:].bitcast(FP8X4),
@@ -158,38 +135,24 @@ def tile_picked_embpos_none_p_kernel(tc, x_words, x_scales, w1, w2_words, w2_sca
                     stop=True,
                 )
             if last:
-                res = [keep.tile([P, width], F32, name=f"res_last{u}", align_bytes=64) for u in range(2)]
-                nc.scalar.copy(out=res[0][:], in_=accs[0])
-                nc.scalar.dma_start(out=out_rows[:, 0, start : start + width], in_=res[0][:])
-                nc.vector.tensor_copy(out=res[1][:], in_=accs[1])
-                nc.sync.dma_start(out=out_rows[:, 1, start : start + width], in_=res[1][:])
-            elif width > GROUP:
-                for u in range(2):
-                    res = keep.tile([P, width], F32, name=f"res_wide{u}", align_bytes=64)
-                    nc.scalar.copy(out=res[:], in_=accs[u])
-                    nc.sync.dma_start(out=out_rows[:, u, start : start + width], in_=res[:])
+                upper = keep.tile([P, width], F32, name="res_upper", align_bytes=64)
+                lower = keep.tile([P, width], F32, name="res_lower", align_bytes=64)
+                nc.scalar.copy(out=upper[:], in_=halves[0])
+                nc.scalar.dma_start(out=out_rows[:, 0, start : start + width], in_=upper[:])
+                nc.vector.tensor_copy(out=lower[:], in_=halves[1])
+                nc.sync.dma_start(out=out_rows[:, 1, start : start + width], in_=lower[:])
             else:
                 res = keep.tile([P, 2, width], F32, name=f"res{start}", align_bytes=64)
                 nc.scalar.copy(out=res[:], in_=both[:])
                 nc.sync.dma_start(out=out_rows[:, :, start : start + width], in_=res[:])
 
-        for g in range(groups - 1):
-            gather(g)
-        for a in range(2):
-            nc.vector.quantize_mx(out=w1_codes[a][:].bitcast(FP8X4), scales=w1_plane[a][:], in_=w1_bf[:, 2 * a : 2 * a + 2, :, :].rearrange("p t m j -> p (t m j)"))
-        gather(groups - 1)
         for c in range(BANKS):
             project(c)
-        add_pos(0)
-        add_pos(1)
-        add_pos(2)
-        layer2(*PIECES[0])
-        add_pos(3)
-        add_pos(4)
-        layer2(*PIECES[1])
-        add_pos(5)
-        add_pos(6)
-        layer2(*PIECES[2])
-        add_pos(7)
-        layer2(*PIECES[3])
-        layer2(*PIECES[4])
+        for c in range(chunks):
+            add_pos(c)
+            for start, width in PIECES:
+                if start + width == c * CHUNK:
+                    second_layer(start, width)
+            if c + BANKS < chunks:
+                project(c + BANKS)
+        second_layer(*PIECES[-1])

@@ -19,8 +19,12 @@ P = 128
 PACK = 4
 QUADRANT = 32
 BLOCKS = K // 32
+SPREAD = P // BLOCKS
+W1_AT = (3584, 15104)
+POS_AT = (9216, 0, 4864, 15104)
 LIST_ROWS = 16
-W_HALF = H // 2
+W_FIRST = 128
+W_VECTOR = 128
 GROUP = 256
 CHUNK = 128
 BANKS = 4
@@ -39,42 +43,50 @@ def tile_picked_embpos_none_p_kernel(tc, x_words, x_scales, w1, w2_words, w2_sca
         offsets = keep.tile([P, S // LIST_ROWS], U16, name="offsets")
         nc.sync.dma_start(offsets[:], offs)
 
-        xs_table = keep.tile([P, T], U8, name="xs_table", align_bytes=64)
+        shared = ctx.enter_context(tc.tile_pool(name="shared", bufs=1))
+        xs_table = shared.tile([P, T], U8, name="xs_table", align_bytes=64, offset=POS_AT[0])
         nc.vector.memset(xs_table[:].bitcast(I32), 0)
-        w2_plane = keep.tile([P, N], U8, name="w2_plane", align_bytes=64)
-        nc.vector.memset(w2_plane[:].bitcast(I32), 0)
+        xs_plane = keep.tile([P, S], U8, name="xs_plane", align_bytes=64)
+        nc.vector.memset(xs_plane[:].bitcast(I32), 0)
 
         def load_plane(plane, scales):
             for r in range(4):
                 nc.sync.dma_start(out=plane[r:P:QUADRANT, :].bitcast(I32), in_=scales[0, r:BLOCKS:4, :].bitcast(I32))
 
         w1_rows = w1.rearrange("(p j) c -> p j c", j=PACK)
-        w1_raw = [keep.tile([P, PACK, W_HALF], F32, name=f"w1_raw{half}", align_bytes=64) for half in range(2)]
-        nc.sync.dma_start(out=w1_raw[0][:], in_=w1_rows[:, :, :W_HALF])
-        load_plane(xs_table, x_scales)
-        nc.sync.dma_start(out=w1_raw[1][:], in_=w1_rows[:, :, W_HALF:])
+        w1_raw = [shared.tile([P, PACK, (W_FIRST, H - W_FIRST)[half]], F32, name=f"w1_raw{half}", align_bytes=64, offset=W1_AT[half]) for half in range(2)]
+        nc.sync.dma_start(out=w1_raw[0][:], in_=w1_rows[:, :, :W_FIRST])
+        nc.sync.dma_start(out=xs_table[0:P:SPREAD, :].bitcast(I32), in_=x_scales[0].bitcast(I32))
+        nc.sync.dma_start(out=w1_raw[1][:], in_=w1_rows[:, :, W_FIRST:])
         xw_table = keep.tile([P, T], U32, name="xw_table", align_bytes=64)
         nc.sync.dma_start(out=xw_table[:].bitcast(I32), in_=x_words[0].rearrange("p n t -> p (n t)").bitcast(I32))
 
         pos_rows = pos.rearrange("(p t) s -> p t s", t=PACK)
-        pos_sb = [keep.tile([P, PACK, GROUP], F32, name=f"pos{g}", align_bytes=64) for g in range(groups)]
-        w2_codes = keep.tile([P, 2 * N], U8, name="w2_codes", align_bytes=64)
-        for g in range(groups):
-            if g == groups // 2:
+
+        xs_picked = keep.tile([P, S], U8, name="xs_picked", align_bytes=64)
+        nc.vector.tensor_copy(xs_picked[:], xs_table[:].indirect(offsets[:]))
+        for r in range(4):
+            nc.sync.dma_start(out=xs_plane[r:P:QUADRANT, :].bitcast(I32), in_=xs_picked[SPREAD * r : P : QUADRANT, :].bitcast(I32))
+        pos_sb = [shared.tile([P, PACK, GROUP], F32, name="pos0", align_bytes=64, offset=POS_AT[0])]
+        nc.sync.dma_start(out=pos_sb[0][:], in_=pos_rows[:, :, :GROUP])
+
+        w1_bf = keep.tile([P, PACK, P, PACK], BF16, name="w1_bf", align_bytes=64)
+        dealt = w1_bf[:].rearrange("p (a e) m j -> p a m j e", e=2)
+        rows = [raw[:].rearrange("p j (m a e) -> p a m j e", a=2, e=2) for raw in w1_raw]
+        m_first, m_scalar = W_FIRST // PACK, (H - W_VECTOR) // PACK
+        nc.scalar.copy(out=dealt[:, :, :m_first], in_=rows[0])
+        nc.scalar.copy(out=dealt[:, :, m_first:m_scalar], in_=rows[1][:, :, : m_scalar - m_first])
+        nc.vector.tensor_copy(out=dealt[:, :, m_scalar:], in_=rows[1][:, :, m_scalar - m_first :])
+        w2_codes = shared.tile([P, 2 * N], U8, name="w2_codes", align_bytes=64, offset=4096)
+        w2_plane = shared.tile([P, N], U8, name="w2_plane", align_bytes=64, offset=4608)
+        nc.vector.memset(w2_plane[:].bitcast(I32), 0)
+        for g in range(1, groups):
+            pos_sb.append(shared.tile([P, PACK, GROUP], F32, name=f"pos{g}", align_bytes=64, offset=POS_AT[g]))
+            if g == groups - 1:
                 nc.sync.dma_start(out=w2_codes[:].bitcast(I32), in_=w2_words[0].bitcast(I32))
                 load_plane(w2_plane, w2_scales)
             nc.sync.dma_start(out=pos_sb[g][:], in_=pos_rows[:, :, g * GROUP : (g + 1) * GROUP])
 
-        xs_picked = keep.tile([P, S], U8, name="xs_picked", align_bytes=64)
-        nc.vector.tensor_copy(xs_picked[:], xs_table[:].indirect(offsets[:]))
-
-        w1_bf = keep.tile([P, PACK, P, PACK], BF16, name="w1_bf", align_bytes=64)
-        m_half = W_HALF // PACK
-        for half in range(2):
-            nc.scalar.copy(
-                out=w1_bf[:, :, half * m_half : (half + 1) * m_half, :].rearrange("p (a e) m j -> p a m j e", e=2),
-                in_=w1_raw[half][:].rearrange("p j (m a e) -> p a m j e", a=2, e=2),
-            )
         w1_codes = keep.tile([P, H], U32, name="w1_codes", align_bytes=64)
         w1_plane = keep.tile([P, H], U8, name="w1_plane", align_bytes=64)
         nc.vector.quantize_mx(out=w1_codes[:].bitcast(FP8X4), scales=w1_plane[:], in_=w1_bf[:].rearrange("p t m j -> p (t m j)"))
@@ -98,7 +110,7 @@ def tile_picked_embpos_none_p_kernel(tc, x_words, x_scales, w1, w2_words, w2_sca
                     lhsT=w1_codes[:, t * P : (t + 1) * P].bitcast(FP8X4),
                     lhsT_scale=w1_plane[:, t * P : (t + 1) * P],
                     rhs=xw_picked[g][:, lo : lo + CHUNK].bitcast(FP8X4),
-                    rhs_scale=xs_picked[:, c * CHUNK : (c + 1) * CHUNK],
+                    rhs_scale=xs_plane[:, c * CHUNK : (c + 1) * CHUNK],
                     start=True,
                     stop=True,
                 )

@@ -20,11 +20,11 @@ PACK = 4
 QUADRANT = 32
 BLOCKS = K // 32
 SPREAD = P // BLOCKS
-W1_AT = (3584, 15104)
-POS_AT = (9216, 0, 4864, 15104)
+W1_AT = (5632, 11008)
+POS_AT = (0, 0, 6912, 11008)
+POS_LOADS = ((0, 128), (128, 384), (512, 256), (768, 256))
 LIST_ROWS = 16
-W_FIRST = 128
-W_VECTOR = 128
+M_SCALAR = 104
 GROUP = 256
 CHUNK = 128
 BANKS = 4
@@ -44,7 +44,7 @@ def tile_picked_embpos_none_p_kernel(tc, x_words, x_scales, w1, w2_words, w2_sca
         nc.sync.dma_start(offsets[:], offs)
 
         shared = ctx.enter_context(tc.tile_pool(name="shared", bufs=1))
-        xs_table = shared.tile([P, T], U8, name="xs_table", align_bytes=64, offset=POS_AT[0])
+        xs_table = keep.tile([P, T], U8, name="xs_table", align_bytes=64)
         nc.vector.memset(xs_table[:].bitcast(I32), 0)
         xs_plane = keep.tile([P, S], U8, name="xs_plane", align_bytes=64)
         nc.vector.memset(xs_plane[:].bitcast(I32), 0)
@@ -54,42 +54,50 @@ def tile_picked_embpos_none_p_kernel(tc, x_words, x_scales, w1, w2_words, w2_sca
                 nc.sync.dma_start(out=plane[r:P:QUADRANT, :].bitcast(I32), in_=scales[0, r:BLOCKS:4, :].bitcast(I32))
 
         w1_rows = w1.rearrange("(p j) c -> p j c", j=PACK)
-        w1_raw = [shared.tile([P, PACK, (W_FIRST, H - W_FIRST)[half]], F32, name=f"w1_raw{half}", align_bytes=64, offset=W1_AT[half]) for half in range(2)]
-        nc.sync.dma_start(out=w1_raw[0][:], in_=w1_rows[:, :, :W_FIRST])
+        w1_raw = [shared.tile([P, (1, PACK - 1)[half], H], F32, name=f"w1_raw{half}", align_bytes=64, offset=W1_AT[half]) for half in range(2)]
+        nc.sync.dma_start(out=w1_raw[0][:], in_=w1_rows[:, :1, :])
         nc.sync.dma_start(out=xs_table[0:P:SPREAD, :].bitcast(I32), in_=x_scales[0].bitcast(I32))
-        nc.sync.dma_start(out=w1_raw[1][:], in_=w1_rows[:, :, W_FIRST:])
+        nc.sync.dma_start(out=w1_raw[1][:], in_=w1_rows[:, 1:, :])
         xw_table = keep.tile([P, T], U32, name="xw_table", align_bytes=64)
         nc.sync.dma_start(out=xw_table[:].bitcast(I32), in_=x_words[0].rearrange("p n t -> p (n t)").bitcast(I32))
 
         pos_rows = pos.rearrange("(p t) s -> p t s", t=PACK)
+        pos_sb = [keep.tile([P, PACK, CHUNK], F32, name="pos0", align_bytes=64)]
+        nc.sync.dma_start(out=pos_sb[0][:], in_=pos_rows[:, :, :CHUNK])
 
         xs_picked = keep.tile([P, S], U8, name="xs_picked", align_bytes=64)
         nc.vector.tensor_copy(xs_picked[:], xs_table[:].indirect(offsets[:]))
         for r in range(4):
             nc.sync.dma_start(out=xs_plane[r:P:QUADRANT, :].bitcast(I32), in_=xs_picked[SPREAD * r : P : QUADRANT, :].bitcast(I32))
-        pos_sb = [shared.tile([P, PACK, GROUP], F32, name="pos0", align_bytes=64, offset=POS_AT[0])]
-        nc.sync.dma_start(out=pos_sb[0][:], in_=pos_rows[:, :, :GROUP])
 
         w1_bf = keep.tile([P, PACK, P, PACK], BF16, name="w1_bf", align_bytes=64)
         dealt = w1_bf[:].rearrange("p (a e) m j -> p a m j e", e=2)
         rows = [raw[:].rearrange("p j (m a e) -> p a m j e", a=2, e=2) for raw in w1_raw]
-        m_first, m_scalar = W_FIRST // PACK, (H - W_VECTOR) // PACK
-        nc.scalar.copy(out=dealt[:, :, :m_first], in_=rows[0])
-        nc.scalar.copy(out=dealt[:, :, m_first:m_scalar], in_=rows[1][:, :, : m_scalar - m_first])
-        nc.vector.tensor_copy(out=dealt[:, :, m_scalar:], in_=rows[1][:, :, m_scalar - m_first :])
-        w2_codes = shared.tile([P, 2 * N], U8, name="w2_codes", align_bytes=64, offset=4096)
-        w2_plane = shared.tile([P, N], U8, name="w2_plane", align_bytes=64, offset=4608)
+        nc.scalar.copy(out=dealt[:, :, :M_SCALAR, :1], in_=rows[0][:, :, :M_SCALAR])
+        nc.vector.tensor_copy(out=dealt[:, :, M_SCALAR:, :1], in_=rows[0][:, :, M_SCALAR:])
+        nc.vector.tensor_copy(out=dealt[:, :, M_SCALAR:, 1:], in_=rows[1][:, :, M_SCALAR:])
+        for a in range(2):
+            nc.scalar.copy(out=dealt[:, a, :M_SCALAR, 1:], in_=rows[1][:, a, :M_SCALAR])
+        w2_codes = shared.tile([P, 2 * N], U8, name="w2_codes", align_bytes=64, offset=6144)
+        w2_plane = shared.tile([P, N], U8, name="w2_plane", align_bytes=64, offset=6656)
         nc.vector.memset(w2_plane[:].bitcast(I32), 0)
         for g in range(1, groups):
-            pos_sb.append(shared.tile([P, PACK, GROUP], F32, name=f"pos{g}", align_bytes=64, offset=POS_AT[g]))
+            start, width = POS_LOADS[g]
+            pos_sb.append(shared.tile([P, PACK, width], F32, name=f"pos{g}", align_bytes=64, offset=POS_AT[g]))
             if g == groups - 1:
                 nc.sync.dma_start(out=w2_codes[:].bitcast(I32), in_=w2_words[0].bitcast(I32))
                 load_plane(w2_plane, w2_scales)
-            nc.sync.dma_start(out=pos_sb[g][:], in_=pos_rows[:, :, g * GROUP : (g + 1) * GROUP])
+            nc.sync.dma_start(out=pos_sb[g][:], in_=pos_rows[:, :, start : start + width])
 
         w1_codes = keep.tile([P, H], U32, name="w1_codes", align_bytes=64)
         w1_plane = keep.tile([P, H], U8, name="w1_plane", align_bytes=64)
-        nc.vector.quantize_mx(out=w1_codes[:].bitcast(FP8X4), scales=w1_plane[:], in_=w1_bf[:].rearrange("p t m j -> p (t m j)"))
+        for a in range(2):
+            cols = slice(2 * a * P, 2 * (a + 1) * P)
+            nc.vector.quantize_mx(
+                out=w1_codes[:, cols].bitcast(FP8X4),
+                scales=w1_plane[:, cols],
+                in_=w1_bf[:, 2 * a : 2 * a + 2].rearrange("p t m j -> p (t m j)"),
+            )
 
         xw_picked = [keep.tile([P, GROUP], U32, name=f"xw_picked{g}", align_bytes=64) for g in range(groups)]
         list_cols = GROUP // LIST_ROWS
@@ -116,7 +124,8 @@ def tile_picked_embpos_none_p_kernel(tc, x_words, x_scales, w1, w2_words, w2_sca
                 )
 
         def add_pos(c):
-            g, lo = divmod(c * CHUNK, GROUP)
+            g = max(n for n in range(len(POS_LOADS)) if POS_LOADS[n][0] <= c * CHUNK)
+            lo = c * CHUNK - POS_LOADS[g][0]
             start = max(first for first, width in PIECES if first <= c * CHUNK)
             at = (c * CHUNK - start) * PACK
             nc.vector.tensor_tensor(

@@ -20,11 +20,10 @@ PACK = 4
 QUADRANT = 32
 BLOCKS = K // 32
 SPREAD = P // BLOCKS
-W1_AT = (5632, 11008)
 POS_AT = (0, 0, 6912, 11008)
 POS_LOADS = ((0, 128), (128, 384), (512, 256), (768, 256))
 LIST_ROWS = 16
-M_SCALAR = 104
+M_SCALAR = 48
 GROUP = 256
 CHUNK = 128
 BANKS = 4
@@ -44,7 +43,7 @@ def tile_picked_embpos_none_p_kernel(tc, x_words, x_scales, w1, w2_words, w2_sca
         nc.sync.dma_start(offsets[:], offs)
 
         shared = ctx.enter_context(tc.tile_pool(name="shared", bufs=1))
-        xs_table = keep.tile([P, T], U8, name="xs_table", align_bytes=64)
+        xs_table = shared.tile([P, T], U8, name="xs_table", align_bytes=64, offset=5632)
         nc.vector.memset(xs_table[:].bitcast(I32), 0)
         xs_plane = keep.tile([P, S], U8, name="xs_plane", align_bytes=64)
         nc.vector.memset(xs_plane[:].bitcast(I32), 0)
@@ -54,10 +53,10 @@ def tile_picked_embpos_none_p_kernel(tc, x_words, x_scales, w1, w2_words, w2_sca
                 nc.sync.dma_start(out=plane[r:P:QUADRANT, :].bitcast(I32), in_=scales[0, r:BLOCKS:4, :].bitcast(I32))
 
         w1_rows = w1.rearrange("(p j) c -> p j c", j=PACK)
-        w1_raw = [shared.tile([P, (1, PACK - 1)[half], H], F32, name=f"w1_raw{half}", align_bytes=64, offset=W1_AT[half]) for half in range(2)]
-        nc.sync.dma_start(out=w1_raw[0][:], in_=w1_rows[:, :1, :])
+        w1_raw = shared.tile([P, PACK, H], F32, name="w1_raw", align_bytes=64, offset=11008)
+        nc.sync.dma_start(out=w1_raw[:, :1, :], in_=w1_rows[:, :1, :])
         nc.sync.dma_start(out=xs_table[0:P:SPREAD, :].bitcast(I32), in_=x_scales[0].bitcast(I32))
-        nc.sync.dma_start(out=w1_raw[1][:], in_=w1_rows[:, 1:, :])
+        nc.sync.dma_start(out=w1_raw[:, 1:, :], in_=w1_rows[:, 1:, :])
         xw_table = keep.tile([P, T], U32, name="xw_table", align_bytes=64)
         nc.sync.dma_start(out=xw_table[:].bitcast(I32), in_=x_words[0].rearrange("p n t -> p (n t)").bitcast(I32))
 
@@ -72,12 +71,11 @@ def tile_picked_embpos_none_p_kernel(tc, x_words, x_scales, w1, w2_words, w2_sca
 
         w1_bf = keep.tile([P, PACK, P, PACK], BF16, name="w1_bf", align_bytes=64)
         dealt = w1_bf[:].rearrange("p (a e) m j -> p a m j e", e=2)
-        rows = [raw[:].rearrange("p j (m a e) -> p a m j e", a=2, e=2) for raw in w1_raw]
-        nc.scalar.copy(out=dealt[:, :, :M_SCALAR, :1], in_=rows[0][:, :, :M_SCALAR])
-        nc.vector.tensor_copy(out=dealt[:, :, M_SCALAR:, :1], in_=rows[0][:, :, M_SCALAR:])
-        nc.vector.tensor_copy(out=dealt[:, :, M_SCALAR:, 1:], in_=rows[1][:, :, M_SCALAR:])
-        for a in range(2):
-            nc.scalar.copy(out=dealt[:, a, :M_SCALAR, 1:], in_=rows[1][:, a, :M_SCALAR])
+        rows = w1_raw[:].rearrange("p j (m a e) -> p a m j e", a=2, e=2)
+        nc.scalar.copy(out=dealt[:, 1, :M_SCALAR, :1], in_=rows[:, 1, :M_SCALAR, :1])
+        nc.scalar.copy(out=dealt[:, 0], in_=rows[:, 0])
+        nc.scalar.copy(out=dealt[:, 1, :M_SCALAR, 1:], in_=rows[:, 1, :M_SCALAR, 1:])
+        nc.vector.tensor_copy(out=dealt[:, 1, M_SCALAR:], in_=rows[:, 1, M_SCALAR:])
         w2_codes = shared.tile([P, 2 * N], U8, name="w2_codes", align_bytes=64, offset=6144)
         w2_plane = shared.tile([P, N], U8, name="w2_plane", align_bytes=64, offset=6656)
         nc.vector.memset(w2_plane[:].bitcast(I32), 0)

@@ -27,7 +27,9 @@ M_SCALAR = 48
 GROUP = 256
 CHUNK = 128
 BANKS = 4
-PIECES = ((0, 256), (256, 256), (512, 256), (768, 128), (896, 128))
+PIECES = ((0, 256), (256, 128), (384, 256), (640, 128), (768, 128), (896, 128))
+GATHERS = ((0, 256), (256, 256), (512, 512))
+STORES = ((0, 384), (384, 256), (640, 128), (768, 128))
 
 
 def tile_picked_embpos_none_p_kernel(tc, x_words, x_scales, w1, w2_words, w2_scales, pos, offs, out):
@@ -97,17 +99,17 @@ def tile_picked_embpos_none_p_kernel(tc, x_words, x_scales, w1, w2_words, w2_sca
                 in_=w1_bf[:, 2 * a : 2 * a + 2].rearrange("p t m j -> p (t m j)"),
             )
 
-        xw_picked = [keep.tile([P, GROUP], U32, name=f"xw_picked{g}", align_bytes=64) for g in range(groups)]
-        list_cols = GROUP // LIST_ROWS
-        for g in range(groups):
-            nc.vector.tensor_copy(xw_picked[g][:], xw_table[:].indirect(offsets[:, g * list_cols : (g + 1) * list_cols]))
+        xw_picked = {start: keep.tile([P, width], U32, name=f"xw_picked{start}", align_bytes=64) for start, width in GATHERS}
+        for start, width in GATHERS:
+            nc.vector.tensor_copy(xw_picked[start][:], xw_table[:].indirect(offsets[:, start // LIST_ROWS : (start + width) // LIST_ROWS]))
 
         h_bf = {start: keep.tile([P, width * PACK], BF16, name=f"h_bf{start}", align_bytes=64) for start, width in PIECES}
         out_rows = out.rearrange("(u p) s -> p u s", p=P)
         projected = []
 
         def project(c):
-            g, lo = divmod(c * CHUNK, GROUP)
+            g = max(first for first, width in GATHERS if first <= c * CHUNK)
+            lo = c * CHUNK - g
             acc1 = psum1.tile([P, PACK, CHUNK], F32, name="acc1")
             projected.append(acc1)
             for t in range(PACK):
@@ -132,6 +134,11 @@ def tile_picked_embpos_none_p_kernel(tc, x_words, x_scales, w1, w2_words, w2_sca
                 pos_sb[g][:, :, lo : lo + CHUNK].rearrange("p t (n i) -> p n t i", i=2),
                 ADD,
             )
+
+        results = {}
+
+        def next_store(start):
+            return max(store for store in STORES if store[0] <= start)
 
         def second_layer(start, width):
             h_codes = keep.tile([P, width], U32, name=f"h_codes{start}", align_bytes=64)
@@ -161,9 +168,12 @@ def tile_picked_embpos_none_p_kernel(tc, x_words, x_scales, w1, w2_words, w2_sca
                 nc.vector.tensor_copy(out=lower[:], in_=halves[1])
                 nc.sync.dma_start(out=out_rows[:, 1, start : start + width], in_=lower[:])
             else:
-                res = keep.tile([P, 2, width], F32, name=f"res{start}", align_bytes=64)
-                nc.scalar.copy(out=res[:], in_=both[:])
-                nc.sync.dma_start(out=out_rows[:, :, start : start + width], in_=res[:])
+                first, wide = next_store(start)
+                if start == first:
+                    results[first] = keep.tile([P, 2, wide], F32, name=f"res{first}", align_bytes=64)
+                nc.scalar.copy(out=results[first][:, :, start - first : start - first + width], in_=both[:])
+                if start + width == first + wide:
+                    nc.sync.dma_start(out=out_rows[:, :, first : first + wide], in_=results[first][:])
 
         for c in range(BANKS):
             project(c)

@@ -27,6 +27,9 @@ M_SCALAR = 48
 GROUP = 256
 CHUNK = 128
 BANKS = 4
+BANK_BYTES = 2048
+FIRST_BANKS = (0, 1, 2, 3, 0, 1, 2, 4)
+SECOND_BANKS = {0: (4,), 256: (5,), 384: (6,), 640: (7,), 768: (3,), 896: (5, 0)}
 PIECES = ((0, 256), (256, 128), (384, 256), (640, 128), (768, 128), (896, 128))
 GATHERS = ((0, 256), (256, 256), (512, 512))
 STORES = ((0, 384), (384, 256), (640, 128), (768, 128))
@@ -38,14 +41,13 @@ def tile_picked_embpos_none_p_kernel(tc, x_words, x_scales, w1, w2_words, w2_sca
     chunks = S // CHUNK
     with ExitStack() as ctx:
         keep = ctx.enter_context(tc.tile_pool(name="keep", bufs=1))
-        psum1 = ctx.enter_context(tc.psum_pool(name="psum1", bufs=BANKS))
-        psum2 = ctx.enter_context(tc.psum_pool(name="psum2", bufs=BANKS))
+        psum = ctx.enter_context(tc.psum_pool(name="psum", bufs=1))
 
         offsets = keep.tile([P, S // LIST_ROWS], U16, name="offsets")
         nc.sync.dma_start(offsets[:], offs)
 
         shared = ctx.enter_context(tc.tile_pool(name="shared", bufs=1))
-        xs_table = shared.tile([P, T], U8, name="xs_table", align_bytes=64, offset=5632)
+        xs_table = shared.tile([P, T], U8, name="xs_table", align_bytes=64, offset=4864)
         nc.vector.memset(xs_table[:].bitcast(I32), 0)
         xs_plane = keep.tile([P, S], U8, name="xs_plane", align_bytes=64)
         nc.vector.memset(xs_plane[:].bitcast(I32), 0)
@@ -55,7 +57,7 @@ def tile_picked_embpos_none_p_kernel(tc, x_words, x_scales, w1, w2_words, w2_sca
                 nc.sync.dma_start(out=plane[r:P:QUADRANT, :].bitcast(I32), in_=scales[0, r:BLOCKS:4, :].bitcast(I32))
 
         w1_rows = w1.rearrange("(p j) c -> p j c", j=PACK)
-        w1_raw = shared.tile([P, PACK, H], F32, name="w1_raw", align_bytes=64, offset=11008)
+        w1_raw = shared.tile([P, PACK, H], F32, name="w1_raw", align_bytes=64, offset=6912)
         nc.sync.dma_start(out=w1_raw[:, :1, :], in_=w1_rows[:, :1, :])
         nc.sync.dma_start(out=xs_table[0:P:SPREAD, :].bitcast(I32), in_=x_scales[0].bitcast(I32))
         nc.sync.dma_start(out=w1_raw[:, 1:, :], in_=w1_rows[:, 1:, :])
@@ -84,7 +86,7 @@ def tile_picked_embpos_none_p_kernel(tc, x_words, x_scales, w1, w2_words, w2_sca
         for g in range(1, groups):
             start, width = POS_LOADS[g]
             pos_sb.append(shared.tile([P, PACK, width], F32, name=f"pos{g}", align_bytes=64, offset=POS_AT[g]))
-            if g == groups - 1:
+            if g == groups // 2:
                 nc.sync.dma_start(out=w2_codes[:].bitcast(I32), in_=w2_words[0].bitcast(I32))
                 load_plane(w2_plane, w2_scales)
             nc.sync.dma_start(out=pos_sb[g][:], in_=pos_rows[:, :, start : start + width])
@@ -110,7 +112,7 @@ def tile_picked_embpos_none_p_kernel(tc, x_words, x_scales, w1, w2_words, w2_sca
         def project(c):
             g = max(first for first, width in GATHERS if first <= c * CHUNK)
             lo = c * CHUNK - g
-            acc1 = psum1.tile([P, PACK, CHUNK], F32, name="acc1")
+            acc1 = psum.tile([P, PACK, CHUNK], F32, name=f"acc1_{c}", offset=FIRST_BANKS[c] * BANK_BYTES)
             projected.append(acc1)
             for t in range(PACK):
                 nc.tensor.matmul_mx(
@@ -146,9 +148,9 @@ def tile_picked_embpos_none_p_kernel(tc, x_words, x_scales, w1, w2_words, w2_sca
             nc.vector.quantize_mx(out=h_codes[:].bitcast(FP8X4), scales=h_plane[:], in_=h_bf[start][:])
             last = start + width == S
             if last:
-                halves = [psum2.tile([P, width], F32, name="acc2")[:] for u in range(2)]
+                halves = [psum.tile([P, width], F32, name=f"acc2_{start}_{u}", offset=SECOND_BANKS[start][u] * BANK_BYTES)[:] for u in range(2)]
             else:
-                both = psum2.tile([P, 2, width], F32, name="acc2")
+                both = psum.tile([P, 2, width], F32, name=f"acc2_{start}", offset=SECOND_BANKS[start][0] * BANK_BYTES)
                 halves = [both[:, u, :] for u in range(2)]
             for u in range(2):
                 nc.tensor.matmul_mx(

@@ -20,8 +20,8 @@ PACK = 4
 QUADRANT = 32
 BLOCKS = K // 32
 SPREAD = P // BLOCKS
-POS_AT = (0, 0, 6912, 11008)
-POS_LOADS = ((0, 128), (128, 384), (512, 256), (768, 256))
+POS_AT = (0, 832, 5696, 9792, 13888)
+POS_LOADS = ((0, 128), (128, 256), (384, 256), (640, 256), (896, 128))
 LIST_ROWS = 16
 M_SCALAR = 48
 GROUP = 256
@@ -29,15 +29,14 @@ CHUNK = 128
 BANKS = 4
 BANK_BYTES = 2048
 FIRST_BANKS = (0, 1, 2, 3, 0, 1, 2, 4)
-SECOND_BANKS = {0: (4,), 256: (5,), 384: (6,), 640: (7,), 768: (3,), 896: (5, 0)}
-PIECES = ((0, 256), (256, 128), (384, 256), (640, 128), (768, 128), (896, 128))
+SECOND_BANKS = {0: (4,), 256: (5,), 512: (6,), 640: (7,), 768: (3,), 896: (5, 0)}
+PIECES = ((0, 256), (256, 256), (512, 128), (640, 128), (768, 128), (896, 128))
 GATHERS = ((0, 256), (256, 256), (512, 512))
-STORES = ((0, 384), (384, 256), (640, 128), (768, 128))
+STORES = ((0, 256), (256, 384), (640, 128), (768, 128))
 
 
 def tile_picked_embpos_none_p_kernel(tc, x_words, x_scales, w1, w2_words, w2_scales, pos, offs, out):
     nc = tc.nc
-    groups = S // GROUP
     chunks = S // CHUNK
     with ExitStack() as ctx:
         keep = ctx.enter_context(tc.tile_pool(name="keep", bufs=1))
@@ -57,7 +56,7 @@ def tile_picked_embpos_none_p_kernel(tc, x_words, x_scales, w1, w2_words, w2_sca
                 nc.sync.dma_start(out=plane[r:P:QUADRANT, :].bitcast(I32), in_=scales[0, r:BLOCKS:4, :].bitcast(I32))
 
         w1_rows = w1.rearrange("(p j) c -> p j c", j=PACK)
-        w1_raw = shared.tile([P, PACK, H], F32, name="w1_raw", align_bytes=64, offset=6912)
+        w1_raw = shared.tile([P, PACK, H], F32, name="w1_raw", align_bytes=64, offset=9792)
         nc.sync.dma_start(out=w1_raw[:, :1, :], in_=w1_rows[:, :1, :])
         nc.sync.dma_start(out=xs_table[0:P:SPREAD, :].bitcast(I32), in_=x_scales[0].bitcast(I32))
         nc.sync.dma_start(out=w1_raw[:, 1:, :], in_=w1_rows[:, 1:, :])
@@ -80,13 +79,13 @@ def tile_picked_embpos_none_p_kernel(tc, x_words, x_scales, w1, w2_words, w2_sca
         nc.scalar.copy(out=dealt[:, 0], in_=rows[:, 0])
         nc.scalar.copy(out=dealt[:, 1, :M_SCALAR, 1:], in_=rows[:, 1, :M_SCALAR, 1:])
         nc.vector.tensor_copy(out=dealt[:, 1, M_SCALAR:], in_=rows[:, 1, M_SCALAR:])
-        w2_codes = shared.tile([P, 2 * N], U8, name="w2_codes", align_bytes=64, offset=6144)
-        w2_plane = shared.tile([P, N], U8, name="w2_plane", align_bytes=64, offset=6656)
+        w2_codes = shared.tile([P, 2 * N], U8, name="w2_codes", align_bytes=64, offset=4928)
+        w2_plane = shared.tile([P, N], U8, name="w2_plane", align_bytes=64, offset=5440)
         nc.vector.memset(w2_plane[:].bitcast(I32), 0)
-        for g in range(1, groups):
+        for g in range(1, len(POS_LOADS)):
             start, width = POS_LOADS[g]
             pos_sb.append(shared.tile([P, PACK, width], F32, name=f"pos{g}", align_bytes=64, offset=POS_AT[g]))
-            if g == groups // 2:
+            if g == 3:
                 nc.sync.dma_start(out=w2_codes[:].bitcast(I32), in_=w2_words[0].bitcast(I32))
                 load_plane(w2_plane, w2_scales)
             nc.sync.dma_start(out=pos_sb[g][:], in_=pos_rows[:, :, start : start + width])
@@ -146,6 +145,10 @@ def tile_picked_embpos_none_p_kernel(tc, x_words, x_scales, w1, w2_words, w2_sca
             h_codes = keep.tile([P, width], U32, name=f"h_codes{start}", align_bytes=64)
             h_plane = keep.tile([P, width], U8, name=f"h_plane{start}", align_bytes=64)
             nc.vector.quantize_mx(out=h_codes[:].bitcast(FP8X4), scales=h_plane[:], in_=h_bf[start][:])
+            for lo in range(0, width, GROUP):
+                multiply(h_codes, h_plane, lo, start + lo, min(GROUP, width - lo))
+
+        def multiply(h_codes, h_plane, lo, start, width):
             last = start + width == S
             if last:
                 halves = [psum.tile([P, width], F32, name=f"acc2_{start}_{u}", offset=SECOND_BANKS[start][u] * BANK_BYTES)[:] for u in range(2)]
@@ -157,18 +160,16 @@ def tile_picked_embpos_none_p_kernel(tc, x_words, x_scales, w1, w2_words, w2_sca
                     out=halves[u],
                     lhsT=w2_codes[:, 2 * u * P : 2 * (u + 1) * P].bitcast(FP4X4),
                     lhsT_scale=w2_plane[:, u * P : (u + 1) * P],
-                    rhs=h_codes[:].bitcast(FP8X4),
-                    rhs_scale=h_plane[:],
+                    rhs=h_codes[:, lo : lo + width].bitcast(FP8X4),
+                    rhs_scale=h_plane[:, lo : lo + width],
                     start=True,
                     stop=True,
                 )
             if last:
-                upper = keep.tile([P, width], F32, name="res_upper", align_bytes=64)
-                lower = keep.tile([P, width], F32, name="res_lower", align_bytes=64)
-                nc.scalar.copy(out=upper[:], in_=halves[0])
-                nc.scalar.dma_start(out=out_rows[:, 0, start : start + width], in_=upper[:])
-                nc.vector.tensor_copy(out=lower[:], in_=halves[1])
-                nc.sync.dma_start(out=out_rows[:, 1, start : start + width], in_=lower[:])
+                res_last = keep.tile([P, 2, width], F32, name="res_last", align_bytes=64)
+                nc.scalar.copy(out=res_last[:, 0, :], in_=halves[0])
+                nc.vector.tensor_copy(out=res_last[:, 1, :], in_=halves[1])
+                nc.sync.dma_start(out=out_rows[:, :, start : start + width], in_=res_last[:])
             else:
                 first, wide = next_store(start)
                 if start == first:

@@ -20,19 +20,18 @@ PACK = 4
 QUADRANT = 32
 BLOCKS = K // 32
 SPREAD = P // BLOCKS
-POS_AT = (0, 832, 5696, 9792, 13888)
+POS_AT = {1: 0, 2: 4864, 3: 12352, 4: 16448}
 POS_LOADS = ((0, 128), (128, 256), (384, 256), (640, 256), (896, 128))
 LIST_ROWS = 16
-M_SCALAR = 48
 GROUP = 256
 CHUNK = 128
 BANKS = 4
 BANK_BYTES = 2048
-FIRST_BANKS = (0, 1, 2, 3, 0, 1, 2, 4)
-SECOND_BANKS = {0: (4,), 256: (5,), 512: (6,), 640: (7,), 768: (3,), 896: (5, 0)}
+FIRST_BANKS = (0, 1, 2, 3, 0, 1, 2, 3)
+SECOND_BANKS = {0: (4,), 256: (5,), 512: (6,), 640: (7,), 768: (4,), 896: (5, 0)}
 PIECES = ((0, 256), (256, 256), (512, 128), (640, 128), (768, 128), (896, 128))
 GATHERS = ((0, 256), (256, 256), (512, 512))
-STORES = ((0, 256), (256, 384), (640, 128), (768, 128))
+STORES = ((0, 256), (256, 256), (512, 128), (640, 128), (768, 128))
 
 
 def tile_picked_embpos_none_p_kernel(tc, x_words, x_scales, w1, w2_words, w2_scales, pos, offs, out):
@@ -46,49 +45,50 @@ def tile_picked_embpos_none_p_kernel(tc, x_words, x_scales, w1, w2_words, w2_sca
         nc.sync.dma_start(offsets[:], offs)
 
         shared = ctx.enter_context(tc.tile_pool(name="shared", bufs=1))
-        xs_table = shared.tile([P, T], U8, name="xs_table", align_bytes=64, offset=4864)
-        nc.vector.memset(xs_table[:].bitcast(I32), 0)
+        xs_table = keep.tile([P, T], U8, name="xs_table", align_bytes=64)
+        nc.sync.dma_start(out=xs_table[BLOCKS : 2 * BLOCKS, :].bitcast(I32), in_=x_scales[0].bitcast(I32))
+        for first, last in ((0, BLOCKS), (32, 64), (64, P)):
+            nc.vector.memset(xs_table[first:last, :].bitcast(I32), 0)
         xs_plane = keep.tile([P, S], U8, name="xs_plane", align_bytes=64)
         nc.vector.memset(xs_plane[:].bitcast(I32), 0)
 
-        def load_plane(plane, scales):
-            for r in range(4):
-                nc.sync.dma_start(out=plane[r:P:QUADRANT, :].bitcast(I32), in_=scales[0, r:BLOCKS:4, :].bitcast(I32))
-
         w1_rows = w1.rearrange("(p j) c -> p j c", j=PACK)
-        w1_raw = shared.tile([P, PACK, H], F32, name="w1_raw", align_bytes=64, offset=9792)
-        nc.sync.dma_start(out=w1_raw[:, :1, :], in_=w1_rows[:, :1, :])
-        nc.sync.dma_start(out=xs_table[0:P:SPREAD, :].bitcast(I32), in_=x_scales[0].bitcast(I32))
-        nc.sync.dma_start(out=w1_raw[:, 1:, :], in_=w1_rows[:, 1:, :])
+        w1_raw = shared.tile([P, PACK, H], F32, name="w1_raw", align_bytes=64, offset=4032)
+        nc.sync.dma_start(out=w1_raw[:], in_=w1_rows)
         xw_table = keep.tile([P, T], U32, name="xw_table", align_bytes=64)
         nc.sync.dma_start(out=xw_table[:].bitcast(I32), in_=x_words[0].rearrange("p n t -> p (n t)").bitcast(I32))
 
         pos_rows = pos.rearrange("(p t) s -> p t s", t=PACK)
-        pos_sb = [keep.tile([P, PACK, CHUNK], F32, name="pos0", align_bytes=64)]
-        nc.sync.dma_start(out=pos_sb[0][:], in_=pos_rows[:, :, :CHUNK])
+        pos_sb = []
+
+        def load_pos(g):
+            start, width = POS_LOADS[g]
+            if g in POS_AT:
+                pos_sb.append(shared.tile([P, PACK, width], F32, name=f"pos{g}", align_bytes=64, offset=POS_AT[g]))
+            else:
+                pos_sb.append(keep.tile([P, PACK, width], F32, name=f"pos{g}", align_bytes=64))
+            nc.sync.dma_start(out=pos_sb[g][:], in_=pos_rows[:, :, start : start + width])
+
+        load_pos(0)
 
         xs_picked = keep.tile([P, S], U8, name="xs_picked", align_bytes=64)
         nc.vector.tensor_copy(xs_picked[:], xs_table[:].indirect(offsets[:]))
         for r in range(4):
-            nc.sync.dma_start(out=xs_plane[r:P:QUADRANT, :].bitcast(I32), in_=xs_picked[SPREAD * r : P : QUADRANT, :].bitcast(I32))
+            nc.scalar.dma_start(out=xs_plane[r:P:QUADRANT, :].bitcast(I32), in_=xs_picked[BLOCKS + r : 2 * BLOCKS : 4, :].bitcast(I32))
 
-        w1_bf = keep.tile([P, PACK, P, PACK], BF16, name="w1_bf", align_bytes=64)
+        w1_bf = shared.tile([P, PACK, P, PACK], BF16, name="w1_bf", align_bytes=64, offset=16384)
         dealt = w1_bf[:].rearrange("p (a e) m j -> p a m j e", e=2)
         rows = w1_raw[:].rearrange("p j (m a e) -> p a m j e", a=2, e=2)
-        nc.scalar.copy(out=dealt[:, 1, :M_SCALAR, :1], in_=rows[:, 1, :M_SCALAR, :1])
-        nc.scalar.copy(out=dealt[:, 0], in_=rows[:, 0])
-        nc.scalar.copy(out=dealt[:, 1, :M_SCALAR, 1:], in_=rows[:, 1, :M_SCALAR, 1:])
-        nc.vector.tensor_copy(out=dealt[:, 1, M_SCALAR:], in_=rows[:, 1, M_SCALAR:])
-        w2_codes = shared.tile([P, 2 * N], U8, name="w2_codes", align_bytes=64, offset=4928)
-        w2_plane = shared.tile([P, N], U8, name="w2_plane", align_bytes=64, offset=5440)
+        for a in range(2):
+            nc.vector.tensor_copy(out=dealt[:, a], in_=rows[:, a])
+        load_pos(1)
+        load_pos(2)
+        w2_codes = shared.tile([P, 2 * N], U8, name="w2_codes", align_bytes=64, offset=4096)
+        w2_plane = shared.tile([P, N], U8, name="w2_plane", align_bytes=64, offset=4608)
         nc.vector.memset(w2_plane[:].bitcast(I32), 0)
-        for g in range(1, len(POS_LOADS)):
-            start, width = POS_LOADS[g]
-            pos_sb.append(shared.tile([P, PACK, width], F32, name=f"pos{g}", align_bytes=64, offset=POS_AT[g]))
-            if g == 3:
-                nc.sync.dma_start(out=w2_codes[:].bitcast(I32), in_=w2_words[0].bitcast(I32))
-                load_plane(w2_plane, w2_scales)
-            nc.sync.dma_start(out=pos_sb[g][:], in_=pos_rows[:, :, start : start + width])
+        nc.sync.dma_start(out=w2_codes[:].bitcast(I32), in_=w2_words[0].bitcast(I32))
+        for r in range(4):
+            nc.sync.dma_start(out=w2_plane[r:P:QUADRANT, :].bitcast(I32), in_=w2_scales[0, r:BLOCKS:4, :].bitcast(I32))
 
         w1_codes = keep.tile([P, H], U32, name="w1_codes", align_bytes=64)
         w1_plane = keep.tile([P, H], U8, name="w1_plane", align_bytes=64)
@@ -99,6 +99,9 @@ def tile_picked_embpos_none_p_kernel(tc, x_words, x_scales, w1, w2_words, w2_sca
                 scales=w1_plane[:, cols],
                 in_=w1_bf[:, 2 * a : 2 * a + 2].rearrange("p t m j -> p (t m j)"),
             )
+
+        load_pos(3)
+        load_pos(4)
 
         xw_picked = {start: keep.tile([P, width], U32, name=f"xw_picked{start}", align_bytes=64) for start, width in GATHERS}
         for start, width in GATHERS:

@@ -26,11 +26,12 @@ LIST_ROWS = 16
 GROUP = 256
 CHUNK = 128
 BANKS = 4
+STAGED = 0
 BANK_BYTES = 2048
-FIRST_BANKS = (0, 1, 2, 3, 0, 1, 2, 3)
-SECOND_BANKS = {0: (4,), 256: (5,), 512: (6,), 640: (7,), 768: (4,), 896: (5, 0)}
+FIRST_BANKS = (0, 1, 2, 3, 7, 1, 2, 3)
+SECOND_BANKS = {0: (4,), 256: (5,), 512: (6,), 640: (0,), 768: (4, 1), 896: (5, 7)}
 PIECES = ((0, 256), (256, 256), (512, 128), (640, 128), (768, 128), (896, 128))
-GATHERS = ((0, 256), (256, 256), (512, 512))
+GATHERS = ((0, 128), (128, 384), (512, 512))
 STORES = ((0, 256), (256, 256), (512, 128), (640, 128), (768, 128))
 
 
@@ -132,6 +133,18 @@ def tile_picked_embpos_none_p_kernel(tc, x_words, x_scales, w1, w2_words, w2_sca
             lo = c * CHUNK - POS_LOADS[g][0]
             start = max(first for first, width in PIECES if first <= c * CHUNK)
             at = (c * CHUNK - start) * PACK
+            if c == STAGED:
+                staged = keep.tile([P, CHUNK, PACK], F32, name="staged", align_bytes=64)
+                woven = keep.tile([P, CHUNK, PACK], F32, name="woven", align_bytes=64)
+                nc.scalar.copy(out=woven[:], in_=pos_sb[g][:, :, lo : lo + CHUNK].rearrange("p t s -> p s t"))
+                nc.scalar.copy(out=staged[:], in_=projected[c][:].rearrange("p t s -> p s t"))
+                nc.gpsimd.tensor_tensor(
+                    h_bf[start][:, at : at + CHUNK * PACK],
+                    staged[:].rearrange("p s t -> p (s t)"),
+                    woven[:].rearrange("p s t -> p (s t)"),
+                    ADD,
+                )
+                return
             nc.vector.tensor_tensor(
                 h_bf[start][:, at : at + CHUNK * PACK].rearrange("p (n i t) -> p n t i", i=2, t=PACK),
                 projected[c][:].rearrange("p t (n i) -> p n t i", i=2),
@@ -152,7 +165,7 @@ def tile_picked_embpos_none_p_kernel(tc, x_words, x_scales, w1, w2_words, w2_sca
                 multiply(h_codes, h_plane, lo, start + lo, min(GROUP, width - lo))
 
         def multiply(h_codes, h_plane, lo, start, width):
-            last = start + width == S
+            last = start + width >= S - CHUNK
             if last:
                 halves = [psum.tile([P, width], F32, name=f"acc2_{start}_{u}", offset=SECOND_BANKS[start][u] * BANK_BYTES)[:] for u in range(2)]
             else:
@@ -169,7 +182,7 @@ def tile_picked_embpos_none_p_kernel(tc, x_words, x_scales, w1, w2_words, w2_sca
                     stop=True,
                 )
             if last:
-                res_last = keep.tile([P, 2, width], F32, name="res_last", align_bytes=64)
+                res_last = keep.tile([P, 2, width], F32, name=f"res_last{start}", align_bytes=64)
                 nc.scalar.copy(out=res_last[:, 0, :], in_=halves[0])
                 nc.vector.tensor_copy(out=res_last[:, 1, :], in_=halves[1])
                 nc.sync.dma_start(out=out_rows[:, :, start : start + width], in_=res_last[:])

@@ -20,7 +20,7 @@ PACK = 4
 QUADRANT = 32
 BLOCKS = K // 32
 SPREAD = P // BLOCKS
-POS_AT = {1: 0, 2: 4864, 3: 12352, 4: 16448}
+POS_AT = {1: 0, 2: 4864, 3: 12544, 4: 16640}
 POS_LOADS = ((0, 128), (128, 256), (384, 256), (640, 256), (896, 128))
 LIST_ROWS = 16
 GROUP = 256
@@ -46,17 +46,17 @@ def tile_picked_embpos_none_p_kernel(tc, x_words, x_scales, w1, w2_words, w2_sca
         nc.sync.dma_start(offsets[:], offs)
 
         shared = ctx.enter_context(tc.tile_pool(name="shared", bufs=1))
-        xs_table = keep.tile([P, T], U8, name="xs_table", align_bytes=64)
+        xs_table = keep.tile([P, T], U8, name="xs_table", align_bytes=256)
         nc.sync.dma_start(out=xs_table[BLOCKS : 2 * BLOCKS, :].bitcast(I32), in_=x_scales[0].bitcast(I32))
         for first, last in ((0, BLOCKS), (32, 64), (64, P)):
             nc.vector.memset(xs_table[first:last, :].bitcast(I32), 0)
-        xs_plane = keep.tile([P, S], U8, name="xs_plane", align_bytes=64)
+        xs_plane = keep.tile([P, S], U8, name="xs_plane", align_bytes=256)
         nc.vector.memset(xs_plane[:].bitcast(I32), 0)
 
         w1_rows = w1.rearrange("(p j) c -> p j c", j=PACK)
-        w1_raw = shared.tile([P, PACK, H], F32, name="w1_raw", align_bytes=64, offset=4032)
+        w1_raw = shared.tile([P, PACK, H], F32, name="w1_raw", align_bytes=256, offset=3840)
         nc.sync.dma_start(out=w1_raw[:], in_=w1_rows)
-        xw_table = keep.tile([P, T], U32, name="xw_table", align_bytes=64)
+        xw_table = keep.tile([P, T], U32, name="xw_table", align_bytes=256)
         nc.sync.dma_start(out=xw_table[:].bitcast(I32), in_=x_words[0].rearrange("p n t -> p (n t)").bitcast(I32))
 
         pos_rows = pos.rearrange("(p t) s -> p t s", t=PACK)
@@ -65,14 +65,14 @@ def tile_picked_embpos_none_p_kernel(tc, x_words, x_scales, w1, w2_words, w2_sca
         def load_pos(g):
             start, width = POS_LOADS[g]
             if g in POS_AT:
-                pos_sb.append(shared.tile([P, PACK, width], F32, name=f"pos{g}", align_bytes=64, offset=POS_AT[g]))
+                pos_sb.append(shared.tile([P, PACK, width], F32, name=f"pos{g}", align_bytes=256, offset=POS_AT[g]))
             else:
-                pos_sb.append(keep.tile([P, PACK, width], F32, name=f"pos{g}", align_bytes=64))
+                pos_sb.append(keep.tile([P, PACK, width], F32, name=f"pos{g}", align_bytes=256))
             nc.sync.dma_start(out=pos_sb[g][:], in_=pos_rows[:, :, start : start + width])
 
         load_pos(0)
 
-        xs_picked = keep.tile([P, S], U8, name="xs_picked", align_bytes=64)
+        xs_picked = keep.tile([P, S], U8, name="xs_picked", align_bytes=256)
         nc.vector.tensor_copy(xs_picked[:], xs_table[:].indirect(offsets[:]))
         for r in range(4):
             nc.scalar.dma_start(out=xs_plane[r:P:QUADRANT, :].bitcast(I32), in_=xs_picked[BLOCKS + r : 2 * BLOCKS : 4, :].bitcast(I32))
@@ -84,8 +84,8 @@ def tile_picked_embpos_none_p_kernel(tc, x_words, x_scales, w1, w2_words, w2_sca
             nc.vector.tensor_copy(out=dealt[:, a], in_=rows[:, a])
         load_pos(1)
         load_pos(2)
-        w2_codes = shared.tile([P, 2 * N], U8, name="w2_codes", align_bytes=64, offset=4096)
-        w2_plane = shared.tile([P, N], U8, name="w2_plane", align_bytes=64, offset=4608)
+        w2_codes = shared.tile([P, 2 * N], U8, name="w2_codes", align_bytes=256, offset=4096)
+        w2_plane = shared.tile([P, N], U8, name="w2_plane", align_bytes=256, offset=4608)
         nc.vector.memset(w2_plane[:].bitcast(I32), 0)
         nc.sync.dma_start(out=w2_codes[:].bitcast(I32), in_=w2_words[0].bitcast(I32))
         for r in range(4):
@@ -182,14 +182,14 @@ def tile_picked_embpos_none_p_kernel(tc, x_words, x_scales, w1, w2_words, w2_sca
                     stop=True,
                 )
             if last:
-                res_last = keep.tile([P, 2, width], F32, name=f"res_last{start}", align_bytes=64)
+                res_last = keep.tile([P, 2, width], F32, name=f"res_last{start}", align_bytes=256)
                 nc.scalar.copy(out=res_last[:, 0, :], in_=halves[0])
                 nc.vector.tensor_copy(out=res_last[:, 1, :], in_=halves[1])
                 nc.sync.dma_start(out=out_rows[:, :, start : start + width], in_=res_last[:])
             else:
                 first, wide = next_store(start)
                 if start == first:
-                    results[first] = keep.tile([P, 2, wide], F32, name=f"res{first}", align_bytes=64)
+                    results[first] = keep.tile([P, 2, wide], F32, name=f"res{first}", align_bytes=256)
                 nc.scalar.copy(out=results[first][:, :, start - first : start - first + width], in_=both[:])
                 if start + width == first + wide:
                     nc.sync.dma_start(out=out_rows[:, :, first : first + wide], in_=results[first][:])

@@ -26,7 +26,7 @@ LIST_ROWS = 16
 GROUP = 256
 CHUNK = 128
 BANKS = 4
-STAGED = 0
+GPSIMD_TOKENS = {0: 128, 1: 64}
 BANK_BYTES = 2048
 FIRST_BANKS = (0, 1, 2, 3, 7, 1, 2, 3)
 SECOND_BANKS = {0: (4,), 256: (5,), 512: (6,), 640: (0,), 768: (4, 1), 896: (5, 7)}
@@ -47,11 +47,10 @@ def tile_picked_embpos_none_p_kernel(tc, x_words, x_scales, w1, w2_words, w2_sca
 
         shared = ctx.enter_context(tc.tile_pool(name="shared", bufs=1))
         xs_table = keep.tile([P, T], U8, name="xs_table", align_bytes=256)
-        nc.sync.dma_start(out=xs_table[BLOCKS : 2 * BLOCKS, :].bitcast(I32), in_=x_scales[0].bitcast(I32))
+        nc.scalar.dma_start(out=xs_table[BLOCKS : 2 * BLOCKS, :].bitcast(I32), in_=x_scales[0].bitcast(I32))
         for first, last in ((0, BLOCKS), (32, 64), (64, P)):
             nc.vector.memset(xs_table[first:last, :].bitcast(I32), 0)
         xs_plane = keep.tile([P, S], U8, name="xs_plane", align_bytes=256)
-        nc.vector.memset(xs_plane[:].bitcast(I32), 0)
 
         w1_rows = w1.rearrange("(p j) c -> p j c", j=PACK)
         w1_raw = shared.tile([P, PACK, H], F32, name="w1_raw", align_bytes=256, offset=3840)
@@ -86,7 +85,6 @@ def tile_picked_embpos_none_p_kernel(tc, x_words, x_scales, w1, w2_words, w2_sca
         load_pos(2)
         w2_codes = shared.tile([P, 2 * N], U8, name="w2_codes", align_bytes=256, offset=4096)
         w2_plane = shared.tile([P, N], U8, name="w2_plane", align_bytes=256, offset=4608)
-        nc.vector.memset(w2_plane[:].bitcast(I32), 0)
         nc.sync.dma_start(out=w2_codes[:].bitcast(I32), in_=w2_words[0].bitcast(I32))
         for r in range(4):
             nc.sync.dma_start(out=w2_plane[r:P:QUADRANT, :].bitcast(I32), in_=w2_scales[0, r:BLOCKS:4, :].bitcast(I32))
@@ -133,24 +131,25 @@ def tile_picked_embpos_none_p_kernel(tc, x_words, x_scales, w1, w2_words, w2_sca
             lo = c * CHUNK - POS_LOADS[g][0]
             start = max(first for first, width in PIECES if first <= c * CHUNK)
             at = (c * CHUNK - start) * PACK
-            if c == STAGED:
-                staged = keep.tile([P, CHUNK, PACK], F32, name="staged", align_bytes=64)
-                woven = keep.tile([P, CHUNK, PACK], F32, name="woven", align_bytes=64)
-                nc.scalar.copy(out=woven[:], in_=pos_sb[g][:, :, lo : lo + CHUNK].rearrange("p t s -> p s t"))
-                nc.scalar.copy(out=staged[:], in_=projected[c][:].rearrange("p t s -> p s t"))
+            skip = GPSIMD_TOKENS.get(c, 0)
+            if skip < CHUNK:
+                nc.vector.tensor_tensor(
+                    h_bf[start][:, at + skip * PACK : at + CHUNK * PACK].rearrange("p (n i t) -> p n t i", i=2, t=PACK),
+                    projected[c][:, :, skip:].rearrange("p t (n i) -> p n t i", i=2),
+                    pos_sb[g][:, :, lo + skip : lo + CHUNK].rearrange("p t (n i) -> p n t i", i=2),
+                    ADD,
+                )
+            if skip:
+                staged = keep.tile([P, skip, PACK], F32, name=f"staged{c}", align_bytes=64)
+                woven = keep.tile([P, skip, PACK], F32, name=f"woven{c}", align_bytes=64)
+                nc.scalar.copy(out=woven[:], in_=pos_sb[g][:, :, lo : lo + skip].rearrange("p t s -> p s t"))
+                nc.scalar.copy(out=staged[:], in_=projected[c][:, :, 0:skip].rearrange("p t s -> p s t"))
                 nc.gpsimd.tensor_tensor(
-                    h_bf[start][:, at : at + CHUNK * PACK],
+                    h_bf[start][:, at : at + skip * PACK],
                     staged[:].rearrange("p s t -> p (s t)"),
                     woven[:].rearrange("p s t -> p (s t)"),
                     ADD,
                 )
-                return
-            nc.vector.tensor_tensor(
-                h_bf[start][:, at : at + CHUNK * PACK].rearrange("p (n i t) -> p n t i", i=2, t=PACK),
-                projected[c][:].rearrange("p t (n i) -> p n t i", i=2),
-                pos_sb[g][:, :, lo : lo + CHUNK].rearrange("p t (n i) -> p n t i", i=2),
-                ADD,
-            )
 
         results = {}
 
@@ -158,7 +157,10 @@ def tile_picked_embpos_none_p_kernel(tc, x_words, x_scales, w1, w2_words, w2_sca
             return max(store for store in STORES if store[0] <= start)
 
         def second_layer(start, width):
-            h_codes = keep.tile([P, width], U32, name=f"h_codes{start}", align_bytes=64)
+            if start == 0:
+                h_codes = shared.tile([P, width], U32, name=f"h_codes{start}", align_bytes=256, offset=POS_AT[2])
+            else:
+                h_codes = keep.tile([P, width], U32, name=f"h_codes{start}", align_bytes=64)
             h_plane = keep.tile([P, width], U8, name=f"h_plane{start}", align_bytes=64)
             nc.vector.quantize_mx(out=h_codes[:].bitcast(FP8X4), scales=h_plane[:], in_=h_bf[start][:])
             for lo in range(0, width, GROUP):
@@ -198,9 +200,11 @@ def tile_picked_embpos_none_p_kernel(tc, x_words, x_scales, w1, w2_words, w2_sca
             project(c)
         for c in range(chunks):
             add_pos(c)
-            for start, width in PIECES:
+            for start, width in PIECES[1:]:
                 if start + width == c * CHUNK:
                     second_layer(start, width)
+            if c == 4:
+                second_layer(*PIECES[0])
             if c + BANKS < chunks:
                 project(c + BANKS)
         second_layer(*PIECES[-1])

@@ -26,12 +26,12 @@ LIST_ROWS = 16
 GROUP = 256
 CHUNK = 128
 BANKS = 4
-GPSIMD_TOKENS = {0: 128, 1: 64}
+GPSIMD_TOKENS = {0: 128, 1: 44}
 BANK_BYTES = 2048
-FIRST_BANKS = (0, 1, 2, 3, 7, 1, 2, 3)
-SECOND_BANKS = {0: (4,), 256: (5,), 512: (6,), 640: (0,), 768: (4, 1), 896: (5, 7)}
+FIRST_BANKS = (0, 1, 2, 3, 7, 3, 1, 2)
+SECOND_BANKS = {0: (4,), 256: (5,), 512: (6,), 640: (0,), 768: (4, 3), 896: (5, 7)}
 PIECES = ((0, 256), (256, 256), (512, 128), (640, 128), (768, 128), (896, 128))
-GATHERS = ((0, 128), (128, 384), (512, 512))
+GATHERS = ((0, 128), (128, 128), (256, 256), (512, 512))
 STORES = ((0, 256), (256, 256), (512, 128), (640, 128), (768, 128))
 
 
@@ -108,13 +108,13 @@ def tile_picked_embpos_none_p_kernel(tc, x_words, x_scales, w1, w2_words, w2_sca
 
         h_bf = {start: keep.tile([P, width * PACK], BF16, name=f"h_bf{start}", align_bytes=64) for start, width in PIECES}
         out_rows = out.rearrange("(u p) s -> p u s", p=P)
-        projected = []
+        projected = {}
 
         def project(c):
             g = max(first for first, width in GATHERS if first <= c * CHUNK)
             lo = c * CHUNK - g
             acc1 = psum.tile([P, PACK, CHUNK], F32, name=f"acc1_{c}", offset=FIRST_BANKS[c] * BANK_BYTES)
-            projected.append(acc1)
+            projected[c] = acc1
             for t in range(PACK):
                 nc.tensor.matmul_mx(
                     out=acc1[:, t, :],
@@ -196,15 +196,16 @@ def tile_picked_embpos_none_p_kernel(tc, x_words, x_scales, w1, w2_words, w2_sca
                 if start + width == first + wide:
                     nc.sync.dma_start(out=out_rows[:, :, first : first + wide], in_=results[first][:])
 
-        for c in range(BANKS):
+        for c in range(BANKS + 1):
             project(c)
         for c in range(chunks):
             add_pos(c)
+            for later in range(BANKS + 1, chunks):
+                if FIRST_BANKS[later] == c:
+                    project(later)
             for start, width in PIECES[1:]:
                 if start + width == c * CHUNK:
                     second_layer(start, width)
             if c == 4:
                 second_layer(*PIECES[0])
-            if c + BANKS < chunks:
-                project(c + BANKS)
         second_layer(*PIECES[-1])

@@ -20,19 +20,21 @@ PACK = 4
 QUADRANT = 32
 BLOCKS = K // 32
 SPREAD = P // BLOCKS
-POS_AT = {1: 0, 2: 4864, 3: 12544, 4: 16640}
-POS_LOADS = ((0, 128), (128, 256), (384, 256), (640, 256), (896, 128))
+POS_AT = {1: 0, 2: 4864, 3: 13568, 4: 16640}
+POS_LOADS = ((0, 128), (128, 256), (384, 320), (704, 192), (896, 128))
 LIST_ROWS = 16
 GROUP = 256
 CHUNK = 128
 BANKS = 4
-GPSIMD_TOKENS = {0: 128, 1: 44}
+SHARE = 32
+LATE_SHARE = 64
+H_AT = 20480
 BANK_BYTES = 2048
-FIRST_BANKS = (0, 1, 2, 3, 7, 3, 1, 2)
-SECOND_BANKS = {0: (4,), 256: (5,), 512: (6,), 640: (0,), 768: (4, 3), 896: (5, 7)}
-PIECES = ((0, 256), (256, 256), (512, 128), (640, 128), (768, 128), (896, 128))
-GATHERS = ((0, 128), (128, 128), (256, 256), (512, 512))
-STORES = ((0, 256), (256, 256), (512, 128), (640, 128), (768, 128))
+FIRST_BANKS = (0, 1, 2, 3, 7, 1, 3, 2)
+SECOND_BANKS = {0: (4,), 256: (5,), 512: (6,), 768: (0,), 640: (4, 1), 896: (5, 7)}
+H_TILES = ((0, 256), (256, 256), (512, 128), (640, 128), (768, 128), (896, 128))
+GATHERS = ((0, 128), (128, 384), (512, 512))
+STORES = H_TILES
 
 
 def tile_picked_embpos_none_p_kernel(tc, x_words, x_scales, w1, w2_words, w2_scales, pos, offs, out):
@@ -46,14 +48,14 @@ def tile_picked_embpos_none_p_kernel(tc, x_words, x_scales, w1, w2_words, w2_sca
         nc.sync.dma_start(offsets[:], offs)
 
         shared = ctx.enter_context(tc.tile_pool(name="shared", bufs=1))
-        xs_table = keep.tile([P, T], U8, name="xs_table", align_bytes=256)
+        xs_table = shared.tile([P, T], U8, name="xs_table", align_bytes=256, offset=0)
         nc.scalar.dma_start(out=xs_table[BLOCKS : 2 * BLOCKS, :].bitcast(I32), in_=x_scales[0].bitcast(I32))
         for first, last in ((0, BLOCKS), (32, 64), (64, P)):
             nc.vector.memset(xs_table[first:last, :].bitcast(I32), 0)
         xs_plane = keep.tile([P, S], U8, name="xs_plane", align_bytes=256)
 
         w1_rows = w1.rearrange("(p j) c -> p j c", j=PACK)
-        w1_raw = shared.tile([P, PACK, H], F32, name="w1_raw", align_bytes=256, offset=3840)
+        w1_raw = shared.tile([P, PACK, H], F32, name="w1_raw", align_bytes=256, offset=4096)
         nc.sync.dma_start(out=w1_raw[:], in_=w1_rows)
         xw_table = keep.tile([P, T], U32, name="xw_table", align_bytes=256)
         nc.sync.dma_start(out=xw_table[:].bitcast(I32), in_=x_words[0].rearrange("p n t -> p (n t)").bitcast(I32))
@@ -74,7 +76,7 @@ def tile_picked_embpos_none_p_kernel(tc, x_words, x_scales, w1, w2_words, w2_sca
         xs_picked = keep.tile([P, S], U8, name="xs_picked", align_bytes=256)
         nc.vector.tensor_copy(xs_picked[:], xs_table[:].indirect(offsets[:]))
         for r in range(4):
-            nc.scalar.dma_start(out=xs_plane[r:P:QUADRANT, :].bitcast(I32), in_=xs_picked[BLOCKS + r : 2 * BLOCKS : 4, :].bitcast(I32))
+            nc.sync.dma_start(out=xs_plane[r:P:QUADRANT, :].bitcast(I32), in_=xs_picked[BLOCKS + r : 2 * BLOCKS : 4, :].bitcast(I32))
 
         w1_bf = shared.tile([P, PACK, P, PACK], BF16, name="w1_bf", align_bytes=64, offset=16384)
         dealt = w1_bf[:].rearrange("p (a e) m j -> p a m j e", e=2)
@@ -106,106 +108,127 @@ def tile_picked_embpos_none_p_kernel(tc, x_words, x_scales, w1, w2_words, w2_sca
         for start, width in GATHERS:
             nc.vector.tensor_copy(xw_picked[start][:], xw_table[:].indirect(offsets[:, start // LIST_ROWS : (start + width) // LIST_ROWS]))
 
-        h_bf = {start: keep.tile([P, width * PACK], BF16, name=f"h_bf{start}", align_bytes=64) for start, width in PIECES}
+        h_bf = {start: keep.tile([P, width * PACK], BF16, name=f"h_bf{start}", align_bytes=64) for start, width in H_TILES if start not in (512, 640)}
+        for start in (512, 640):
+            h_bf[start] = shared.tile([P, dict(H_TILES)[start] * PACK], BF16, name=f"h_bf{start}", align_bytes=256, offset=H_AT)
+        h_plane = {start: keep.tile([P, width], U8, name=f"h_plane{start}", align_bytes=64) for start, width in H_TILES}
+        h_codes = {start: keep.tile([P, width], U32, name=f"h_codes{start}", align_bytes=64) for start, width in H_TILES[1:]}
+        h_codes[0] = shared.tile([P, H_TILES[0][1]], U32, name="h_codes0", align_bytes=256, offset=POS_AT[2])
+        results = {start: keep.tile([P, 2, width], F32, name=f"result{start}", align_bytes=256) for start, width in STORES}
         out_rows = out.rearrange("(u p) s -> p u s", p=P)
         projected = {}
 
+        def holder(ranges, token):
+            start = max(first for first, width in ranges if first <= token)
+            return start, token - start
+
         def project(c):
-            g = max(first for first, width in GATHERS if first <= c * CHUNK)
-            lo = c * CHUNK - g
-            acc1 = psum.tile([P, PACK, CHUNK], F32, name=f"acc1_{c}", offset=FIRST_BANKS[c] * BANK_BYTES)
-            projected[c] = acc1
+            start, lo = holder(GATHERS, c * CHUNK)
+            projected[c] = psum.tile([P, PACK, CHUNK], F32, name=f"acc1_{c}", offset=FIRST_BANKS[c] * BANK_BYTES)
             for t in range(PACK):
                 nc.tensor.matmul_mx(
-                    out=acc1[:, t, :],
+                    out=projected[c][:, t, :],
                     lhsT=w1_codes[:, t * P : (t + 1) * P].bitcast(FP8X4),
                     lhsT_scale=w1_plane[:, t * P : (t + 1) * P],
-                    rhs=xw_picked[g][:, lo : lo + CHUNK].bitcast(FP8X4),
+                    rhs=xw_picked[start][:, lo : lo + CHUNK].bitcast(FP8X4),
                     rhs_scale=xs_plane[:, c * CHUNK : (c + 1) * CHUNK],
                     start=True,
                     stop=True,
                 )
 
-        def add_pos(c):
-            g = max(n for n in range(len(POS_LOADS)) if POS_LOADS[n][0] <= c * CHUNK)
-            lo = c * CHUNK - POS_LOADS[g][0]
-            start = max(first for first, width in PIECES if first <= c * CHUNK)
-            at = (c * CHUNK - start) * PACK
-            skip = GPSIMD_TOKENS.get(c, 0)
-            if skip < CHUNK:
-                nc.vector.tensor_tensor(
-                    h_bf[start][:, at + skip * PACK : at + CHUNK * PACK].rearrange("p (n i t) -> p n t i", i=2, t=PACK),
-                    projected[c][:, :, skip:].rearrange("p t (n i) -> p n t i", i=2),
-                    pos_sb[g][:, :, lo + skip : lo + CHUNK].rearrange("p t (n i) -> p n t i", i=2),
-                    ADD,
-                )
-            if skip:
-                staged = keep.tile([P, skip, PACK], F32, name=f"staged{c}", align_bytes=64)
-                woven = keep.tile([P, skip, PACK], F32, name=f"woven{c}", align_bytes=64)
-                nc.scalar.copy(out=woven[:], in_=pos_sb[g][:, :, lo : lo + skip].rearrange("p t s -> p s t"))
-                nc.scalar.copy(out=staged[:], in_=projected[c][:, :, 0:skip].rearrange("p t s -> p s t"))
-                nc.gpsimd.tensor_tensor(
-                    h_bf[start][:, at : at + skip * PACK],
-                    staged[:].rearrange("p s t -> p (s t)"),
-                    woven[:].rearrange("p s t -> p (s t)"),
-                    ADD,
-                )
+        def summands(token, count):
+            c, skip = divmod(token, CHUNK)
+            load, lo = holder(POS_LOADS, token)
+            tile, at = holder(H_TILES, token)
+            g = [first for first, width in POS_LOADS].index(load)
+            return h_bf[tile][:, at * PACK : (at + count) * PACK], projected[c][:, :, skip : skip + count], pos_sb[g][:, :, lo : lo + count]
 
-        results = {}
+        def add_on_vector(token, count):
+            h_part, product, pos_part = summands(token, count)
+            nc.vector.tensor_tensor(
+                h_part.rearrange("p (n i t) -> p n t i", i=2, t=PACK),
+                product.rearrange("p t (n i) -> p n t i", i=2),
+                pos_part.rearrange("p t (n i) -> p n t i", i=2),
+                ADD,
+            )
 
-        def next_store(start):
-            return max(store for store in STORES if store[0] <= start)
+        laid_out = {}
 
-        def second_layer(start, width):
-            if start == 0:
-                h_codes = shared.tile([P, width], U32, name=f"h_codes{start}", align_bytes=256, offset=POS_AT[2])
+        def lay_out(token, count):
+            h_part, product, pos_part = summands(token, count)
+            staged = keep.tile([P, count, PACK], F32, name=f"staged{token}", align_bytes=64)
+            woven = keep.tile([P, count, PACK], F32, name=f"woven{token}", align_bytes=64)
+            nc.scalar.copy(out=woven[:], in_=pos_part.rearrange("p t s -> p s t"))
+            nc.scalar.copy(out=staged[:], in_=product.rearrange("p t s -> p s t"))
+            laid_out[token] = (h_part, staged, woven)
+
+        def add_on_gpsimd(token):
+            h_part, staged, woven = laid_out[token]
+            nc.gpsimd.tensor_tensor(h_part, staged[:].rearrange("p s t -> p (s t)"), woven[:].rearrange("p s t -> p (s t)"), ADD)
+
+        def quantise(token, count):
+            tile, at = holder(H_TILES, token)
+            nc.vector.quantize_mx(
+                out=h_codes[tile][:, at : at + count].bitcast(FP8X4),
+                scales=h_plane[tile][:, at : at + count],
+                in_=h_bf[tile][:, at * PACK : (at + count) * PACK],
+            )
+
+        def second_layer(token, count):
+            width = max(count, CHUNK)
+            pad = width - count
+            tile, at = holder(H_TILES, token - pad)
+            banks = SECOND_BANKS[token]
+            if len(banks) == 2:
+                halves = [psum.tile([P, width], F32, name=f"acc2_{token}_{u}", offset=banks[u] * BANK_BYTES)[:] for u in range(2)]
             else:
-                h_codes = keep.tile([P, width], U32, name=f"h_codes{start}", align_bytes=64)
-            h_plane = keep.tile([P, width], U8, name=f"h_plane{start}", align_bytes=64)
-            nc.vector.quantize_mx(out=h_codes[:].bitcast(FP8X4), scales=h_plane[:], in_=h_bf[start][:])
-            for lo in range(0, width, GROUP):
-                multiply(h_codes, h_plane, lo, start + lo, min(GROUP, width - lo))
-
-        def multiply(h_codes, h_plane, lo, start, width):
-            last = start + width >= S - CHUNK
-            if last:
-                halves = [psum.tile([P, width], F32, name=f"acc2_{start}_{u}", offset=SECOND_BANKS[start][u] * BANK_BYTES)[:] for u in range(2)]
-            else:
-                both = psum.tile([P, 2, width], F32, name=f"acc2_{start}", offset=SECOND_BANKS[start][0] * BANK_BYTES)
+                both = psum.tile([P, 2, width], F32, name=f"acc2_{token}", offset=banks[0] * BANK_BYTES)
                 halves = [both[:, u, :] for u in range(2)]
             for u in range(2):
                 nc.tensor.matmul_mx(
                     out=halves[u],
                     lhsT=w2_codes[:, 2 * u * P : 2 * (u + 1) * P].bitcast(FP4X4),
                     lhsT_scale=w2_plane[:, u * P : (u + 1) * P],
-                    rhs=h_codes[:, lo : lo + width].bitcast(FP8X4),
-                    rhs_scale=h_plane[:, lo : lo + width],
+                    rhs=h_codes[tile][:, at : at + width].bitcast(FP8X4),
+                    rhs_scale=h_plane[tile][:, at : at + width],
                     start=True,
                     stop=True,
                 )
-            if last:
-                res_last = keep.tile([P, 2, width], F32, name=f"res_last{start}", align_bytes=256)
-                nc.scalar.copy(out=res_last[:, 0, :], in_=halves[0])
-                nc.vector.tensor_copy(out=res_last[:, 1, :], in_=halves[1])
-                nc.sync.dma_start(out=out_rows[:, :, start : start + width], in_=res_last[:])
+            store, lo = holder(STORES, token)
+            result = results[store][:, :, lo : lo + count]
+            if len(banks) == 2:
+                nc.scalar.copy(out=result[:, 0, :], in_=halves[0][:, pad:])
+                nc.vector.tensor_copy(out=result[:, 1, :], in_=halves[1][:, pad:])
             else:
-                first, wide = next_store(start)
-                if start == first:
-                    results[first] = keep.tile([P, 2, wide], F32, name=f"res{first}", align_bytes=256)
-                nc.scalar.copy(out=results[first][:, :, start - first : start - first + width], in_=both[:])
-                if start + width == first + wide:
-                    nc.sync.dma_start(out=out_rows[:, :, first : first + wide], in_=results[first][:])
+                nc.scalar.copy(out=result, in_=both[:, :, pad:])
+            if lo + count == dict(STORES)[store]:
+                nc.sync.dma_start(out=out_rows[:, :, store : store + lo + count], in_=results[store][:])
 
-        for c in range(BANKS + 1):
+        def finish(token, count):
+            quantise(token, count)
+            second_layer(token, count)
+
+        for c in range(5):
             project(c)
-        for c in range(chunks):
-            add_pos(c)
-            for later in range(BANKS + 1, chunks):
-                if FIRST_BANKS[later] == c:
-                    project(later)
-            for start, width in PIECES[1:]:
-                if start + width == c * CHUNK:
-                    second_layer(start, width)
-            if c == 4:
-                second_layer(*PIECES[0])
-        second_layer(*PIECES[-1])
+        lay_out(0, CHUNK)
+        add_on_gpsimd(0)
+        add_on_vector(CHUNK + SHARE, CHUNK - SHARE)
+        lay_out(CHUNK, SHARE)
+        add_on_gpsimd(CHUNK)
+        project(5)
+        lay_out(640, LATE_SHARE)
+        add_on_vector(256, CHUNK)
+        project(7)
+        add_on_vector(384, CHUNK)
+        project(6)
+        add_on_vector(512, CHUNK)
+        finish(256, 256)
+        finish(512, CHUNK)
+        finish(0, 256)
+        add_on_gpsimd(640)
+        add_on_vector(768, CHUNK)
+        add_on_vector(640 + LATE_SHARE, CHUNK - LATE_SHARE)
+        finish(768, CHUNK)
+        add_on_vector(896, CHUNK)
+        finish(640, CHUNK)
+        finish(896, CHUNK)

@@ -101,6 +101,16 @@ def tile_picked_embpos_none_p_kernel(tc, x_words, x_scales, w1, w2_words, w2_sca
                 in_=w1_bf[:, 2 * a : 2 * a + 2].rearrange("p t m j -> p (t m j)"),
             )
 
+        warm = psum.tile([P, H], F32, name="warm", offset=6 * BANK_BYTES)
+        nc.tensor.matmul_mx(
+            out=warm[:],
+            lhsT=w1_codes[:, 0:P].bitcast(FP8X4),
+            lhsT_scale=w1_plane[:, 0:P],
+            rhs=w1_codes[:].bitcast(FP8X4),
+            rhs_scale=w1_plane[:],
+            start=True,
+            stop=True,
+        )
         load_pos(3)
         load_pos(4)
 

@@ -20,20 +20,20 @@ PACK = 4
 QUADRANT = 32
 BLOCKS = K // 32
 SPREAD = P // BLOCKS
-POS_AT = {1: 0, 2: 4864, 3: 13568, 4: 16640}
-POS_LOADS = ((0, 128), (128, 256), (384, 320), (704, 192), (896, 128))
+POS_AT = {1: 20480, 2: 4864, 3: 13568, 4: 16640}
+POS_LOADS = ((0, 64), (64, 320), (384, 320), (704, 192), (896, 128))
 LIST_ROWS = 16
 GROUP = 256
 CHUNK = 128
 BANKS = 4
-SHARE = 32
+SHARE = 40
 LATE_SHARE = 64
-H_AT = 20480
+H_AT = 25600
 BANK_BYTES = 2048
 FIRST_BANKS = (0, 1, 2, 3, 7, 1, 3, 2)
 SECOND_BANKS = {0: (4,), 256: (5,), 512: (6,), 768: (0,), 640: (4, 1), 896: (5, 7)}
 H_TILES = ((0, 256), (256, 256), (512, 128), (640, 128), (768, 128), (896, 128))
-GATHERS = ((0, 128), (128, 384), (512, 512))
+GATHERS = ((0, 128), (128, 128), (256, 256), (512, 512))
 STORES = H_TILES
 
 
@@ -48,7 +48,7 @@ def tile_picked_embpos_none_p_kernel(tc, x_words, x_scales, w1, w2_words, w2_sca
         nc.sync.dma_start(offsets[:], offs)
 
         shared = ctx.enter_context(tc.tile_pool(name="shared", bufs=1))
-        xs_table = shared.tile([P, T], U8, name="xs_table", align_bytes=256, offset=0)
+        xs_table = shared.tile([P, T], U8, name="xs_table", align_bytes=256, offset=POS_AT[1])
         nc.scalar.dma_start(out=xs_table[BLOCKS : 2 * BLOCKS, :].bitcast(I32), in_=x_scales[0].bitcast(I32))
         for first, last in ((0, BLOCKS), (32, 64), (64, P)):
             nc.vector.memset(xs_table[first:last, :].bitcast(I32), 0)
@@ -220,8 +220,9 @@ def tile_picked_embpos_none_p_kernel(tc, x_words, x_scales, w1, w2_words, w2_sca
 
         for c in range(5):
             project(c)
-        lay_out(0, CHUNK)
-        add_on_gpsimd(0)
+        for token in (0, 64):
+            lay_out(token, 64)
+            add_on_gpsimd(token)
         add_on_vector(CHUNK + SHARE, CHUNK - SHARE)
         lay_out(CHUNK, SHARE)
         add_on_gpsimd(CHUNK)

@@ -20,7 +20,7 @@ PACK = 4
 QUADRANT = 32
 BLOCKS = K // 32
 SPREAD = P // BLOCKS
-POS_AT = {1: 20480, 2: 4864, 3: 13568, 4: 16640}
+POS_AT = {1: 45056, 2: 11520, 3: 19712, 4: 17408}
 POS_LOADS = ((0, 64), (64, 320), (384, 320), (704, 192), (896, 128))
 LIST_ROWS = 16
 GROUP = 256
@@ -55,7 +55,7 @@ def tile_picked_embpos_none_p_kernel(tc, x_words, x_scales, w1, w2_words, w2_sca
         xs_plane = keep.tile([P, S], U8, name="xs_plane", align_bytes=256)
 
         w1_rows = w1.rearrange("(p j) c -> p j c", j=PACK)
-        w1_raw = shared.tile([P, PACK, H], F32, name="w1_raw", align_bytes=256, offset=4096)
+        w1_raw = shared.tile([P, PACK, H], F32, name="w1_raw", align_bytes=256, offset=2048)
         nc.sync.dma_start(out=w1_raw[:], in_=w1_rows)
         xw_table = keep.tile([P, T], U32, name="xw_table", align_bytes=256)
         nc.sync.dma_start(out=xw_table[:].bitcast(I32), in_=x_words[0].rearrange("p n t -> p (n t)").bitcast(I32))
@@ -69,14 +69,16 @@ def tile_picked_embpos_none_p_kernel(tc, x_words, x_scales, w1, w2_words, w2_sca
                 pos_sb.append(shared.tile([P, PACK, width], F32, name=f"pos{g}", align_bytes=256, offset=POS_AT[g]))
             else:
                 pos_sb.append(keep.tile([P, PACK, width], F32, name=f"pos{g}", align_bytes=256))
-            nc.sync.dma_start(out=pos_sb[g][:], in_=pos_rows[:, :, start : start + width])
+            queue = nc.scalar if g == 1 else nc.sync
+            queue.dma_start(out=pos_sb[g][:], in_=pos_rows[:, :, start : start + width])
 
         load_pos(0)
 
         xs_picked = keep.tile([P, S], U8, name="xs_picked", align_bytes=256)
         nc.vector.tensor_copy(xs_picked[:], xs_table[:].indirect(offsets[:]))
         for r in range(4):
-            nc.sync.dma_start(out=xs_plane[r:P:QUADRANT, :].bitcast(I32), in_=xs_picked[BLOCKS + r : 2 * BLOCKS : 4, :].bitcast(I32))
+            queue = nc.scalar if r % 2 else nc.sync
+            queue.dma_start(out=xs_plane[r:P:QUADRANT, :].bitcast(I32), in_=xs_picked[BLOCKS + r : 2 * BLOCKS : 4, :].bitcast(I32))
 
         w1_bf = shared.tile([P, PACK, P, PACK], BF16, name="w1_bf", align_bytes=64, offset=16384)
         dealt = w1_bf[:].rearrange("p (a e) m j -> p a m j e", e=2)
@@ -85,8 +87,8 @@ def tile_picked_embpos_none_p_kernel(tc, x_words, x_scales, w1, w2_words, w2_sca
             nc.vector.tensor_copy(out=dealt[:, a], in_=rows[:, a])
         load_pos(1)
         load_pos(2)
-        w2_codes = shared.tile([P, 2 * N], U8, name="w2_codes", align_bytes=256, offset=4096)
-        w2_plane = shared.tile([P, N], U8, name="w2_plane", align_bytes=256, offset=4608)
+        w2_codes = shared.tile([P, 2 * N], U8, name="w2_codes", align_bytes=256, offset=16640)
+        w2_plane = shared.tile([P, N], U8, name="w2_plane", align_bytes=256, offset=17152)
         nc.sync.dma_start(out=w2_codes[:].bitcast(I32), in_=w2_words[0].bitcast(I32))
         for r in range(4):
             nc.sync.dma_start(out=w2_plane[r:P:QUADRANT, :].bitcast(I32), in_=w2_scales[0, r:BLOCKS:4, :].bitcast(I32))

@@ -30,6 +30,7 @@ SHARE = 40
 LATE_SHARE = 64
 H_AT = 25600
 BANK_BYTES = 2048
+WARM_WIDTHS = (512, 512)
 FIRST_BANKS = (0, 1, 2, 3, 7, 1, 3, 2)
 SECOND_BANKS = {0: (4,), 256: (5,), 512: (6,), 768: (0,), 640: (4, 1), 896: (5, 7)}
 H_TILES = ((0, 256), (256, 256), (512, 128), (640, 128), (768, 128), (896, 128))
@@ -103,16 +104,17 @@ def tile_picked_embpos_none_p_kernel(tc, x_words, x_scales, w1, w2_words, w2_sca
                 in_=w1_bf[:, 2 * a : 2 * a + 2].rearrange("p t m j -> p (t m j)"),
             )
 
-        warm = psum.tile([P, H], F32, name="warm", offset=6 * BANK_BYTES)
-        nc.tensor.matmul_mx(
-            out=warm[:],
-            lhsT=w1_codes[:, 0:P].bitcast(FP8X4),
-            lhsT_scale=w1_plane[:, 0:P],
-            rhs=w1_codes[:].bitcast(FP8X4),
-            rhs_scale=w1_plane[:],
-            start=True,
-            stop=True,
-        )
+        warm = psum.tile([P // 2, H], F32, name="warm", offset=6 * BANK_BYTES)
+        for width in WARM_WIDTHS:
+            nc.tensor.matmul_mx(
+                out=warm[:, :width],
+                lhsT=w1_codes[:, : P // 2].bitcast(FP8X4),
+                lhsT_scale=w1_plane[:, : P // 2],
+                rhs=w1_codes[:, :width].bitcast(FP8X4),
+                rhs_scale=w1_plane[:, :width],
+                start=True,
+                stop=True,
+            )
         load_pos(3)
         load_pos(4)
 

@@ -32,7 +32,7 @@ H_AT = 25600
 BANK_BYTES = 2048
 WARM_WIDTHS = (512, 512)
 FIRST_BANKS = (0, 1, 2, 3, 7, 1, 3, 2)
-SECOND_BANKS = {0: (4,), 256: (5,), 512: (6,), 768: (0,), 640: (4, 1), 896: (5, 7)}
+SECOND_BANKS = {0: (7,), 256: (5, 4), 512: (6,), 768: (0,), 640: (4, 1), 896: (5, 7)}
 H_TILES = ((0, 256), (256, 256), (512, 128), (640, 128), (768, 128), (896, 128))
 GATHERS = ((0, 128), (128, 128), (256, 256), (512, 512))
 STORES = H_TILES
@@ -210,7 +210,10 @@ def tile_picked_embpos_none_p_kernel(tc, x_words, x_scales, w1, w2_words, w2_sca
                 )
             store, lo = holder(STORES, token)
             result = results[store][:, :, lo : lo + count]
-            if len(banks) == 2:
+            if token == 256:
+                for u in range(2):
+                    nc.scalar.copy(out=result[:, u, :], in_=halves[u])
+            elif len(banks) == 2:
                 nc.scalar.copy(out=result[:, 0, :], in_=halves[0][:, pad:])
                 nc.vector.tensor_copy(out=result[:, 1, :], in_=halves[1][:, pad:])
             else:

@@ -21,14 +21,15 @@ QUADRANT = 32
 BLOCKS = K // 32
 SPREAD = P // BLOCKS
 POS_AT = {1: 45056, 2: 11520, 3: 19712, 4: 17408}
-POS_LOADS = ((0, 64), (64, 320), (384, 320), (704, 192), (896, 128))
+POS_LOADS = ((0, 128), (128, 256), (384, 320), (704, 192), (896, 128))
 LIST_ROWS = 16
 GROUP = 256
 CHUNK = 128
 BANKS = 4
-SHARE = 40
+SHARE = 56
 LATE_SHARE = 64
 H_AT = 25600
+PICKED_AT = 28672
 BANK_BYTES = 2048
 WARM_WIDTHS = (512, 512)
 FIRST_BANKS = (0, 1, 2, 3, 7, 1, 3, 2)
@@ -118,7 +119,9 @@ def tile_picked_embpos_none_p_kernel(tc, x_words, x_scales, w1, w2_words, w2_sca
         load_pos(3)
         load_pos(4)
 
-        xw_picked = {start: keep.tile([P, width], U32, name=f"xw_picked{start}", align_bytes=64) for start, width in GATHERS}
+        xw_picked = {start: shared.tile([P, width], U32, name=f"xw_picked{start}", align_bytes=256, offset=PICKED_AT + 4 * start) for start, width in GATHERS if start < 256}
+        for start, width in GATHERS[2:]:
+            xw_picked[start] = keep.tile([P, width], U32, name=f"xw_picked{start}", align_bytes=64)
         for start, width in GATHERS:
             nc.vector.tensor_copy(xw_picked[start][:], xw_table[:].indirect(offsets[:, start // LIST_ROWS : (start + width) // LIST_ROWS]))
 
@@ -171,7 +174,10 @@ def tile_picked_embpos_none_p_kernel(tc, x_words, x_scales, w1, w2_words, w2_sca
         def lay_out(token, count):
             h_part, product, pos_part = summands(token, count)
             staged = keep.tile([P, count, PACK], F32, name=f"staged{token}", align_bytes=64)
-            woven = keep.tile([P, count, PACK], F32, name=f"woven{token}", align_bytes=64)
+            if token == CHUNK:
+                woven = shared.tile([P, count, PACK], F32, name=f"woven{token}", align_bytes=256, offset=PICKED_AT + 4 * CHUNK)
+            else:
+                woven = keep.tile([P, count, PACK], F32, name=f"woven{token}", align_bytes=64)
             nc.scalar.copy(out=woven[:], in_=pos_part.rearrange("p t s -> p s t"))
             nc.scalar.copy(out=staged[:], in_=product.rearrange("p t s -> p s t"))
             laid_out[token] = (h_part, staged, woven)

@@ -26,7 +26,7 @@ LIST_ROWS = 16
 GROUP = 256
 CHUNK = 128
 BANKS = 4
-SHARE = 56
+SHARE = 40
 LATE_SHARE = 64
 H_AT = 25600
 PICKED_AT = 28672

@@ -31,7 +31,6 @@ LATE_SHARE = 64
 H_AT = 25600
 PICKED_AT = 28672
 BANK_BYTES = 2048
-WARM_WIDTHS = (512, 512)
 FIRST_BANKS = (0, 1, 2, 3, 7, 1, 3, 2)
 SECOND_BANKS = {0: (7,), 256: (5, 4), 512: (6,), 768: (0,), 640: (4, 1), 896: (5, 7)}
 H_TILES = ((0, 256), (256, 256), (512, 128), (640, 128), (768, 128), (896, 128))
@@ -105,17 +104,6 @@ def tile_picked_embpos_none_p_kernel(tc, x_words, x_scales, w1, w2_words, w2_sca
                 in_=w1_bf[:, 2 * a : 2 * a + 2].rearrange("p t m j -> p (t m j)"),
             )
 
-        warm = psum.tile([P // 2, H], F32, name="warm", offset=6 * BANK_BYTES)
-        for width in WARM_WIDTHS:
-            nc.tensor.matmul_mx(
-                out=warm[:, :width],
-                lhsT=w1_codes[:, : P // 2].bitcast(FP8X4),
-                lhsT_scale=w1_plane[:, : P // 2],
-                rhs=w1_codes[:, :width].bitcast(FP8X4),
-                rhs_scale=w1_plane[:, :width],
-                start=True,
-                stop=True,
-            )
         load_pos(3)
         load_pos(4)
 

from contextlib import ExitStack

import concourse.mybir as mybir

K, T, S, H, N = 512, 2048, 1024, 512, 256
FLOPS = 2 * K * H * S + 2 * H * N * S

F32 = mybir.dt.float32
BF16 = mybir.dt.bfloat16
I32 = mybir.dt.int32
U32 = mybir.dt.uint32
U16 = mybir.dt.uint16
U8 = mybir.dt.uint8
FP8X4 = mybir.dt.float8_e4m3fn_x4
FP4X4 = mybir.dt.float4_e2m1fn_x4
ADD = mybir.AluOpType.add

P = 128
PACK = 4
QUADRANT = 32
BLOCKS = K // 32
SPREAD = P // BLOCKS
POS_AT = {1: 45056, 2: 11520, 3: 19712, 4: 17408}
POS_LOADS = ((0, 128), (128, 256), (384, 320), (704, 192), (896, 128))
LIST_ROWS = 16
GROUP = 256
CHUNK = 128
BANKS = 4
SHARE = 40
LATE_SHARE = 64
H_AT = 25600
PICKED_AT = 28672
BANK_BYTES = 2048
FIRST_BANKS = (0, 1, 2, 3, 7, 1, 3, 2)
SECOND_BANKS = {0: (7,), 256: (5, 4), 512: (6,), 768: (0,), 640: (4, 1), 896: (5, 7)}
H_TILES = ((0, 256), (256, 256), (512, 128), (640, 128), (768, 128), (896, 128))
GATHERS = ((0, 128), (128, 128), (256, 256), (512, 512))
STORES = H_TILES


def tile_picked_embpos_none_p_kernel(tc, x_words, x_scales, w1, w2_words, w2_scales, pos, offs, out):
    nc = tc.nc
    chunks = S // CHUNK
    with ExitStack() as ctx:
        keep = ctx.enter_context(tc.tile_pool(name="keep", bufs=1))
        psum = ctx.enter_context(tc.psum_pool(name="psum", bufs=1))

        offsets = keep.tile([P, S // LIST_ROWS], U16, name="offsets")
        nc.sync.dma_start(offsets[:], offs)

        shared = ctx.enter_context(tc.tile_pool(name="shared", bufs=1))
        xs_table = shared.tile([P, T], U8, name="xs_table", align_bytes=256, offset=POS_AT[1])
        nc.scalar.dma_start(out=xs_table[BLOCKS : 2 * BLOCKS, :].bitcast(I32), in_=x_scales[0].bitcast(I32))
        for first, last in ((0, BLOCKS), (32, 64), (64, P)):
            nc.vector.memset(xs_table[first:last, :].bitcast(I32), 0)
        xs_plane = keep.tile([P, S], U8, name="xs_plane", align_bytes=256)

        w1_rows = w1.rearrange("(p j) c -> p j c", j=PACK)
        w1_raw = shared.tile([P, PACK, H], F32, name="w1_raw", align_bytes=256, offset=2048)
        nc.sync.dma_start(out=w1_raw[:], in_=w1_rows)
        xw_table = keep.tile([P, T], U32, name="xw_table", align_bytes=256)
        nc.sync.dma_start(out=xw_table[:].bitcast(I32), in_=x_words[0].rearrange("p n t -> p (n t)").bitcast(I32))

        pos_rows = pos.rearrange("(p t) s -> p t s", t=PACK)
        pos_sb = []

        def load_pos(g):
            start, width = POS_LOADS[g]
            if g in POS_AT:
                pos_sb.append(shared.tile([P, PACK, width], F32, name=f"pos{g}", align_bytes=256, offset=POS_AT[g]))
            else:
                pos_sb.append(keep.tile([P, PACK, width], F32, name=f"pos{g}", align_bytes=256))
            queue = nc.scalar if g == 1 else nc.sync
            queue.dma_start(out=pos_sb[g][:], in_=pos_rows[:, :, start : start + width])

        load_pos(0)

        xs_picked = keep.tile([P, S], U8, name="xs_picked", align_bytes=256)
        nc.vector.tensor_copy(xs_picked[:], xs_table[:].indirect(offsets[:]))
        for r in range(4):
            queue = nc.scalar if r % 2 else nc.sync
            queue.dma_start(out=xs_plane[r:P:QUADRANT, :].bitcast(I32), in_=xs_picked[BLOCKS + r : 2 * BLOCKS : 4, :].bitcast(I32))

        w1_bf = shared.tile([P, PACK, P, PACK], BF16, name="w1_bf", align_bytes=64, offset=16384)
        dealt = w1_bf[:].rearrange("p (a e) m j -> p a m j e", e=2)
        rows = w1_raw[:].rearrange("p j (m a e) -> p a m j e", a=2, e=2)
        for a in range(2):
            nc.vector.tensor_copy(out=dealt[:, a], in_=rows[:, a])
        load_pos(1)
        load_pos(2)
        w2_codes = shared.tile([P, 2 * N], U8, name="w2_codes", align_bytes=256, offset=16640)
        w2_plane = shared.tile([P, N], U8, name="w2_plane", align_bytes=256, offset=17152)
        nc.sync.dma_start(out=w2_codes[:].bitcast(I32), in_=w2_words[0].bitcast(I32))
        for r in range(4):
            nc.sync.dma_start(out=w2_plane[r:P:QUADRANT, :].bitcast(I32), in_=w2_scales[0, r:BLOCKS:4, :].bitcast(I32))

        w1_codes = keep.tile([P, H], U32, name="w1_codes", align_bytes=64)
        w1_plane = keep.tile([P, H], U8, name="w1_plane", align_bytes=64)
        for a in range(2):
            cols = slice(2 * a * P, 2 * (a + 1) * P)
            nc.vector.quantize_mx(
                out=w1_codes[:, cols].bitcast(FP8X4),
                scales=w1_plane[:, cols],
                in_=w1_bf[:, 2 * a : 2 * a + 2].rearrange("p t m j -> p (t m j)"),
            )

        load_pos(3)
        load_pos(4)

        xw_picked = {start: shared.tile([P, width], U32, name=f"xw_picked{start}", align_bytes=256, offset=PICKED_AT + 4 * start) for start, width in GATHERS if start < 256}
        for start, width in GATHERS[2:]:
            xw_picked[start] = keep.tile([P, width], U32, name=f"xw_picked{start}", align_bytes=64)
        for start, width in GATHERS:
            nc.vector.tensor_copy(xw_picked[start][:], xw_table[:].indirect(offsets[:, start // LIST_ROWS : (start + width) // LIST_ROWS]))

        h_bf = {start: keep.tile([P, width * PACK], BF16, name=f"h_bf{start}", align_bytes=64) for start, width in H_TILES if start not in (512, 640)}
        for start in (512, 640):
            h_bf[start] = shared.tile([P, dict(H_TILES)[start] * PACK], BF16, name=f"h_bf{start}", align_bytes=256, offset=H_AT)
        h_plane = {start: keep.tile([P, width], U8, name=f"h_plane{start}", align_bytes=64) for start, width in H_TILES}
        h_codes = {start: keep.tile([P, width], U32, name=f"h_codes{start}", align_bytes=64) for start, width in H_TILES[1:]}
        h_codes[0] = shared.tile([P, H_TILES[0][1]], U32, name="h_codes0", align_bytes=256, offset=POS_AT[2])
        results = {start: keep.tile([P, 2, width], F32, name=f"result{start}", align_bytes=256) for start, width in STORES}
        out_rows = out.rearrange("(u p) s -> p u s", p=P)
        projected = {}

        def holder(ranges, token):
            start = max(first for first, width in ranges if first <= token)
            return start, token - start

        def project(c):
            start, lo = holder(GATHERS, c * CHUNK)
            projected[c] = psum.tile([P, PACK, CHUNK], F32, name=f"acc1_{c}", offset=FIRST_BANKS[c] * BANK_BYTES)
            for t in range(PACK):
                nc.tensor.matmul_mx(
                    out=projected[c][:, t, :],
                    lhsT=w1_codes[:, t * P : (t + 1) * P].bitcast(FP8X4),
                    lhsT_scale=w1_plane[:, t * P : (t + 1) * P],
                    rhs=xw_picked[start][:, lo : lo + CHUNK].bitcast(FP8X4),
                    rhs_scale=xs_plane[:, c * CHUNK : (c + 1) * CHUNK],
                    start=True,
                    stop=True,
                )

        def summands(token, count):
            c, skip = divmod(token, CHUNK)
            load, lo = holder(POS_LOADS, token)
            tile, at = holder(H_TILES, token)
            g = [first for first, width in POS_LOADS].index(load)
            return h_bf[tile][:, at * PACK : (at + count) * PACK], projected[c][:, :, skip : skip + count], pos_sb[g][:, :, lo : lo + count]

        def add_on_vector(token, count):
            h_part, product, pos_part = summands(token, count)
            nc.vector.tensor_tensor(
                h_part.rearrange("p (n i t) -> p n t i", i=2, t=PACK),
                product.rearrange("p t (n i) -> p n t i", i=2),
                pos_part.rearrange("p t (n i) -> p n t i", i=2),
                ADD,
            )

        laid_out = {}

        def lay_out(token, count):
            h_part, product, pos_part = summands(token, count)
            staged = keep.tile([P, count, PACK], F32, name=f"staged{token}", align_bytes=64)
            if token == CHUNK:
                woven = shared.tile([P, count, PACK], F32, name=f"woven{token}", align_bytes=256, offset=PICKED_AT + 4 * CHUNK)
            else:
                woven = keep.tile([P, count, PACK], F32, name=f"woven{token}", align_bytes=64)
            nc.scalar.copy(out=woven[:], in_=pos_part.rearrange("p t s -> p s t"))
            nc.scalar.copy(out=staged[:], in_=product.rearrange("p t s -> p s t"))
            laid_out[token] = (h_part, staged, woven)

        def add_on_gpsimd(token):
            h_part, staged, woven = laid_out[token]
            nc.gpsimd.tensor_tensor(h_part, staged[:].rearrange("p s t -> p (s t)"), woven[:].rearrange("p s t -> p (s t)"), ADD)

        def quantise(token, count):
            tile, at = holder(H_TILES, token)
            nc.vector.quantize_mx(
                out=h_codes[tile][:, at : at + count].bitcast(FP8X4),
                scales=h_plane[tile][:, at : at + count],
                in_=h_bf[tile][:, at * PACK : (at + count) * PACK],
            )

        def second_layer(token, count):
            width = max(count, CHUNK)
            pad = width - count
            tile, at = holder(H_TILES, token - pad)
            banks = SECOND_BANKS[token]
            if len(banks) == 2:
                halves = [psum.tile([P, width], F32, name=f"acc2_{token}_{u}", offset=banks[u] * BANK_BYTES)[:] for u in range(2)]
            else:
                both = psum.tile([P, 2, width], F32, name=f"acc2_{token}", offset=banks[0] * BANK_BYTES)
                halves = [both[:, u, :] for u in range(2)]
            for u in range(2):
                nc.tensor.matmul_mx(
                    out=halves[u],
                    lhsT=w2_codes[:, 2 * u * P : 2 * (u + 1) * P].bitcast(FP4X4),
                    lhsT_scale=w2_plane[:, u * P : (u + 1) * P],
                    rhs=h_codes[tile][:, at : at + width].bitcast(FP8X4),
                    rhs_scale=h_plane[tile][:, at : at + width],
                    start=True,
                    stop=True,
                )
            store, lo = holder(STORES, token)
            result = results[store][:, :, lo : lo + count]
            if token == 256:
                for u in range(2):
                    nc.scalar.copy(out=result[:, u, :], in_=halves[u])
            elif len(banks) == 2:
                nc.scalar.copy(out=result[:, 0, :], in_=halves[0][:, pad:])
                nc.vector.tensor_copy(out=result[:, 1, :], in_=halves[1][:, pad:])
            else:
                nc.scalar.copy(out=result, in_=both[:, :, pad:])
            if lo + count == dict(STORES)[store]:
                nc.sync.dma_start(out=out_rows[:, :, store : store + lo + count], in_=results[store][:])

        def finish(token, count):
            quantise(token, count)
            second_layer(token, count)

        for c in range(5):
            project(c)
        for token in (0, 64):
            lay_out(token, 64)
            add_on_gpsimd(token)
        add_on_vector(CHUNK + SHARE, CHUNK - SHARE)
        lay_out(CHUNK, SHARE)
        add_on_gpsimd(CHUNK)
        project(5)
        lay_out(640, LATE_SHARE)
        add_on_vector(256, CHUNK)
        project(7)
        add_on_vector(384, CHUNK)
        project(6)
        add_on_vector(512, CHUNK)
        finish(256, 256)
        finish(512, CHUNK)
        finish(0, 256)
        add_on_gpsimd(640)
        add_on_vector(768, CHUNK)
        add_on_vector(640 + LATE_SHARE, CHUNK - LATE_SHARE)
        finish(768, CHUNK)
        add_on_vector(896, CHUNK)
        finish(640, CHUNK)
        finish(896, CHUNK)
